import numpy as np, ml_dtypes
CORES = [1,5,17,21,33,37,49,53]
N = 8
BF = ml_dtypes.bfloat16
def gentries(a):
    return np.ascontiguousarray(a.reshape(8, 16, -1).transpose(0, 2, 1)).reshape(8, -1)
def gtable(e):
    e = np.asarray(e); return np.ascontiguousarray(e.reshape(8, -1, 16).transpose(0, 2, 1)).reshape(128, -1).astype(np.int32)
W, M, L, D, S = 4096, 4096, 64, 32, 5
K = L * D
def cols(rng, n):
    base = rng.integers(0, 256, (N, 8, 1, n)); amp = rng.integers(0, 129, (N, 8, 1, n))
    return np.clip(np.rint(base + amp * (2.0 * rng.random((N, 8, 16, n)) - 1.0)), 0, 255).astype(np.int64)
def parts(rng):
    X, Z = cols(rng, W), cols(rng, L)
    P = rng.integers(0, W, (N, 8, M)); V = rng.integers(0, W, (N, 8, K)); pool = rng.integers(0, M, (N, 8, 256))
    O = np.where(rng.random((N, 8, K)) < 0.5, rng.integers(0, M, (N, 8, K)), np.take_along_axis(pool, rng.integers(0, 256, (N, 8, K)), 2))
    c = rng.random((N, 8, K)); T = np.where(c < 0.45, rng.integers(0, S + 2, (N, 8, K)), np.where(c < 0.85, 99, rng.integers(0, 99, (N, 8, K))))
    return X, Z, P, O, V, T, rng.integers(200, 3400, (N, 8, S))
def pack(X, Z, P, O, V, T, th):
    return {"x": np.ascontiguousarray(X).reshape(N, 128, W).astype(np.float32).astype(BF), "z": np.ascontiguousarray(Z).reshape(N, 128, L).astype(np.float32).astype(BF), "px": P.astype(np.int32),
            "ol": np.stack([gtable(a) for a in O]), "nl": np.stack([gtable(a) for a in V]), "tl": np.stack([gtable(a) for a in T]), "th": th.astype(np.int32)}
def setup_inputs(rng):
    return pack(*parts(rng))
def setup_inputs_spread(rng):
    X = (np.exp2(8 * rng.random((N, 8, 1, W))) * rng.random((N, 8, 16, W))).astype(np.int64); Z = (np.exp2(8 * rng.random((N, 8, 1, L))) * rng.random((N, 8, 16, L))).astype(np.int64)
    e = rng.integers(1, 5, (3, N, 8, 1))
    P = (W * rng.random((N, 8, M)) ** e[0]).astype(np.int64); O = (M * rng.random((N, 8, K)) ** e[1]).astype(np.int64); V = (W * rng.random((N, 8, K)) ** e[2]).astype(np.int64)
    T = np.where(rng.random((N, 8, K)) < 0.3, 99, (100 * rng.random((N, 8, K)) ** 4).astype(np.int64)); th = (4081 * rng.random((N, 8, S)) ** 2).astype(np.int64)
    return pack(X, Z, P, O, V, T, th)
def setup_inputs_ends(rng):
    def ends(n):
        m = rng.integers(0, 3, (N, 8, 1, n)); return np.where(m == 2, 255 * rng.integers(0, 2, (N, 8, 16, n)), 255 * np.minimum(m, 1)) + np.zeros((N, 8, 16, n), np.int64)
    X, Z = ends(W), ends(L); X[..., 0] = 0; X[..., W - 1] = 255
    P = (W - 1) * rng.integers(0, 2, (N, 8, M)); O = (M - 1) * rng.integers(0, 2, (N, 8, K)); V = (W - 1) * rng.integers(0, 2, (N, 8, K)); T = 99 * rng.integers(0, 2, (N, 8, K))
    th = 4080 * rng.integers(0, 2, (N, 8, S)); th[:, 0, 0] = 0; th[:, 1, 0] = 4080; th[0, 7, 0] = 0; th[N - 1, 7, 0] = 4080
    star = int(np.argmax(((37 * np.arange(M)) & (W - 1)) == W - 1))
    for pair, v, n, o, ks in (((0, L - 1), 0, 0, star, (0, 1, D - 1)), ((1, L - 2), 255, W - 1, star, (0, 1, D - 1)), ((2, L - 3), 0, W - 1, M - 1, (0, 3, D - 1))):
        for l in pair:
            Z[..., l] = v
            for k in ks: V[..., k * L + l] = n; T[..., k * L + l] = 0; O[..., k * L + l] = o
    return pack(X, Z, P, O, V, T, th)
def setup_inputs_corners(rng):
    X, Z, P, O, V, T, th = parts(rng)
    th = np.where(rng.random((N, 8, S)) < 0.5, 4080 * rng.integers(0, 2, (N, 8, S)), th)
    for a in range(N):
        ct, cp, co, cv, cz = [rng.permutation(8) for i in range(5)]
        for g in range(8):
            T[a, g] = rng.choice(np.array(((0,), (99,), (98,), (S,), (S - 1,), (0, 98), (1, 2, 99), (0, 1, 2, S - 1, S, S + 1, 98, 99))[ct[g]]), K)
            if cp[g] < 5: P[a, g] = (np.arange(M) & (W - 1), np.zeros(M, np.int64), np.full(M, W - 1), W - 1 - (np.arange(M) & (W - 1)), rng.choice(np.array([0, W - 1]), M))[cp[g]]
            if co[g] < 4: O[a, g] = (np.zeros(K, np.int64), np.full(K, M - 1), rng.choice(np.array([0, M - 1]), K), np.arange(K))[co[g]]
            if cv[g] < 4: V[a, g] = (np.zeros(K, np.int64), np.full(K, W - 1), rng.choice(np.array([0, W - 1]), K), np.arange(K) & (W - 1))[cv[g]]
            if cz[g] < 2: Z[a, g] = 255 * cz[g]
    e = int(rng.integers(0, 8)); X[:, e] = 255; Z[:, e] = 0; Z[:, e, 0, 1::2] = 1; th[:, e, 0] = 4079
    O[:, e, 1::2] = 32 * (M // 32 - 1 - rng.integers(0, 8, (N, K // 2))) + 17
    return pack(X, Z, P, O, V, T, th)
def setup_inputs_crowd(rng):
    X, Z, P, O, V, T, th = parts(rng); pm = rng.permutation(8)
    for g in range(8):
        c = int(pm[g])
        if c < 2: th[:, g] = 4080; T[:, g] = 99
        if c == 2 or c == 3: th[:, g] = 0
        if c == 4 or c == 5: X[:, g, :, 0] = 0; th[:, g] = rng.integers(100, 1500, (N, S))
        for a in range(N):
            one = int(rng.integers(1, L)); p = int(rng.integers(0, M))
            if c == 1: T[a, g, int(rng.integers(0, K))] = 98
            if 2 <= c < 6: O[a, g] = p
            if c == 4 or c == 5:
                V[a, g] = 0; T[a, g] = 0; v = rng.integers(0, 256, 16); v[0] = 255; v[1] = 0
                Z[a, g] = v[np.argsort(rng.random((16, L)), axis=0)]
            if c == 3 or c == 5: O[a, g, one::L] = (p + 1 + int(rng.integers(0, M - 1))) % M
            if c == 5: Z[a, g, :, one] = rng.integers(0, 256, 16)
            if c == 6:
                l = np.arange(K) % L; w = rng.integers(0, M, L); n = int(rng.integers(0, W)); O[a, g] = w[np.minimum(l, L - 1 - l)]; V[a, g] = n; T[a, g] = 0; X[a, g, :, n] = 0
                Z[a, g, 0] = 255; Z[a, g, 15] = 0; v = Z[a, g][:, np.minimum(np.arange(L), L - 1 - np.arange(L))]
                Z[a, g] = np.where(np.arange(L) < L // 2, v, v[::-1])
            if c == 7: O[a, g] = rng.choice(rng.integers(0, M, 4), K)
    return pack(X, Z, P, O, V, T, th)
def setup_inputs_ties(rng):
    X, Z, P, O, V, T, th = parts(rng)
    pat = 64 * rng.integers(0, 4, (N, 8, 16, 8)); X = np.take_along_axis(pat, rng.integers(0, 8, (N, 8, 1, W)), 3)
    Z = np.where(rng.random((N, 8, 1, L)) < 0.5, np.take_along_axis(np.roll(pat, -1, axis=0), rng.integers(0, 8, (N, 8, 1, L)), 3), 64 * rng.integers(0, 4, (N, 8, 16, L)))
    T = np.where(rng.random((N, 8, K)) < 0.7, rng.integers(0, S + 1, (N, 8, K)), 99); th = 64 * rng.integers(0, 40, (N, 8, S)); th[:, ::3, 1] = 0; th[:, 1::3, 0] = 0
    return pack(X, Z, P, O, V, T, th)
def check_inputs(d):
    bad = []
    for k, lo, hi in (("x", 0, 255), ("z", 0, 255), ("px", 0, W - 1), ("ol", 0, M - 1), ("nl", 0, W - 1), ("tl", 0, 99), ("th", 0, 4080)):
        v = np.asarray(d[k]).astype(np.float64)
        if not (np.min(v) >= lo and np.max(v) <= hi): bad.append("range of " + k)
        elif np.any(v != np.floor(v)): bad.append("whole numbers in " + k)
    return bad
def reference(x, z, px, ol, nl, tl, th):
    X = x.astype(np.float32).astype(np.int64).reshape(N, 8, 16, W); Z = z.astype(np.float32).astype(np.int64).reshape(N, 8, 16, L); P = px.astype(np.int64)
    O, V, T = [np.stack([gentries(a) for a in b]).astype(np.int64) for b in (ol, nl, tl)]
    lower = np.tri(L, L, -1, dtype=bool); lane = np.arange(L); A = np.zeros((N, 8, 1), np.int64)
    for s in range(S):
        R = np.where(T <= s, V, np.take_along_axis(P, O, 2))
        y = np.take_along_axis(X, R[:, :, None, :], 3); u = np.add.reduce(np.abs(y - np.tile(Z, (1, 1, 1, D))), axis=2)
        h = (((u * O) >> 5) + u + 37 * O + A) & (W - 1)
        h, O, V, T, Z = [np.roll(a, 1, axis=0) for a in (h, O, V, T, Z)]
        G = np.take_along_axis(X, h[:, :, None, :], 3); d = np.add.reduce(np.abs(G - np.tile(Z, (1, 1, 1, D))), axis=2)
        lim = th[:, :, s:s + 1].astype(np.int64)
        red = (d <= lim) & ~((T > s) & (T < 99))
        V = np.where(red, h, V); T = np.where(red, s + 2, T); A = np.sum(red.astype(np.int64), axis=2, keepdims=True)
        by = d.reshape(N, 8, D, L); j = np.argmax(by, axis=2) * L + lane; b = np.argmin(by, axis=2) * L + lane
        go = np.take_along_axis(d, j, 2) > lim
        np.put_along_axis(T, j, np.where(go, 99, np.take_along_axis(T, j, 2)), 2)
        oj = np.take_along_axis(O, j, 2); hj = np.take_along_axis(h, j, 2); hb = np.take_along_axis(h, b, 2)
        win = go & ~np.any((oj[..., :, None] == oj[..., None, :]) & lower & go[..., None, :], axis=3)
        q, g, l = np.nonzero(win); P[q, g, oj[q, g, l]] = hj[q, g, l]
        Z = (Z + np.take_along_axis(G, b[:, :, None, :], 3)) >> 1
        win = ~np.any((hb[..., :, None] == hb[..., None, :]) & lower, axis=3)
        q, g, l = np.nonzero(win); X[q, g, :, hb[q, g, l]] = Z[q, g, :, l]
    return {"yx": X.reshape(N, 128, W).astype(np.float32).astype(BF), "yp": P.astype(np.float32), "yz": Z.reshape(N, 128, L).astype(np.float32).astype(BF),
            "yn": np.stack([gtable(a) for a in V]).astype(np.float32), "yt": np.stack([gtable(a) for a in T]).astype(np.float32)}

@@ -1,0 +1,466 @@
+from concourse.mybir import AluOpType as ALU, AxisListType, ActivationFunctionType as ACT
+
+S, PADW, DUMP0, TW = 5, 4176, 4097, 256
+BIG = 1.0e6
+
+
+def _sb(n, dtype="float32", p=128):
+    return ("sbuf", [p, n], dtype)
+
+
+SCRATCH = {
+    "XW": _sb(PADW, "bfloat16"), "PW": _sb(PADW, "bfloat16"), "PF": _sb(PADW),
+    "ztb": ("sbuf", [128, 4, TW], "bfloat16"), "ztc": ("sbuf", [128, 4, TW], "bfloat16"),
+    "DF": _sb(2048, "bfloat16"), "AB": _sb(2048, "bfloat16"), "PG": _sb(2048, "bfloat16"),
+    "W": _sb(2048, "bfloat16"), "WP": _sb(2048, "bfloat16"),
+    "pxi": _sb(256, "int32"), "pxt": _sb(512, "int32"), "LH": _sb(512, "bfloat16"),
+    "oli": _sb(128, "int32"), "nli": _sb(128, "int32"), "tli": _sb(128, "int32"),
+    "thi": _sb(5, "int32", 8), "thf": _sb(5, "float32", 8), "GE1": _sb(128, "float32", 8), "GE": _sb(128, "float32", 8),
+    "ones": _sb(128), "oneb": _sb(128, "bfloat16", 1), "CQ": _sb(128, "bfloat16", 1),
+    "G1": _sb(128), "GM": _sb(128), "GL": _sb(128), "LT": _sb(128), "GA": _sb(8), "GP": _sb(8),
+    "mod16": _sb(192), "mod32": _sb(128), "colc": _sb(128), "C2": _sb(128), "SEG16": _sb(192), "SEG32": _sb(128), "DM": _sb(128),
+    "pidx": _sb(1, "int32"), "p16i": _sb(1, "int32"), "p16": _sb(1), "q0": _sb(1), "q1": _sb(1), "wp1": _sb(1), "be1": _sb(1),
+    "beta": _sb(1), "wp": _sb(1), "dump0": _sb(4), "dump": _sb(4), "LM": _sb(5),
+    "OW0": _sb(256), "OW1": _sb(256), "OQ0": _sb(128), "OQ1": _sb(128), "HW": _sb(128), "Q32": _sb(128), "A32": _sb(1), "rs": _sb(1),
+    "MB": _sb(128), "NM": _sb(128), "R1": _sb(128), "RU": _sb(128, "uint16"),
+    "hm": _sb(128), "hv": _sb(128, "int32"), "hs": _sb(128, "int32"),
+    "e1": _sb(128), "e2": _sb(128), "RT0": _sb(128), "RT": _sb(128), "ST": _sb(128), "hN": _sb(128), "K2": _sb(128), "SM": _sb(256),
+    "KI": _sb(8, "int32"), "CI": _sb(12, "int32"), "nogo": _sb(4, "int32"), "gk": _sb(4), "OFF": _sb(12, "uint16"),
+    "GD": _sb(192), "OWN": _sb(192), "HB": _sb(4, "uint16"), "gz": _sb(64), "zi": _sb(64, "int32"),
+    "EP": _sb(64), "FP": _sb(64), "fp": _sb(4), "fpu": _sb(8, "uint16"),
+    "EX": _sb(64), "FX": _sb(64), "fx": _sb(4), "fxu": _sb(8, "uint16"),
+    "hi": _sb(64, "int32"), "ht": _sb(64), "PD": _sb(64, "bfloat16"), "RF": _sb(128),
+    "YN": _sb(128), "YT": _sb(128), "YPg": _sb(256), "LO": _sb(512, "bfloat16"),
+    "ZR": _sb(192 * S, "bfloat16"),
+    "NR": _sb(128 * S),
+    "HS": _sb(128 * S, "uint16"),
+    "HR": _sb(128 * S, "uint16"),
+    "OU": _sb(128 * (S + 1), "uint16"),
+    "ZS": _sb(192 * (S + 1), "bfloat16"),
+    "NS": _sb(128 * (S + 1)),
+}
+for _n in ("pUA", "pUB", "pUC", "pPA", "pPB", "pR", "pM", "pS"):
+    SCRATCH[_n] = ("psum", [128, 512], "float32")
+PIECE = {"%s%d" % (k, s): (k, SCRATCH[k][1][1] // n * s) for k, n in
+         (("ZR", S), ("NR", S), ("HS", S), ("HR", S), ("OU", S + 1), ("ZS", S + 1), ("NS", S + 1)) for s in range(n)}
+RECV = ("rO", "rZ", "rA", "rB", "rC", "rN")
+DMAS = ["d_px", "d_ol", "d_z", "d_tl", "d_nl", "d_th", "d_x", "d_lo", "d_hi",
+        "o_x", "o_lo", "o_hi", "o_pf", "o_p", "o_z", "o_n", "o_t"]
+SEMAPHORES = ["v", "a", "t", "p", "loc"] + ["%s%d" % (k, s) for s in range(S) for k in RECV] + DMAS
+HP = ((0, 64, "pUA", "rA"), (64, 96, "pUB", "rB"), (96, 128, "pUC", "rC"))
+KB = ("pUA", "pUB")
+PB = ("pPA", "pPB")
+
+
+def rank_program(g, core, T, topo):
+    rank = T.rank_of(core)
+    if rank is None:
+        return
+    nxt = T.cores[(rank + 1) % len(T.cores)]
+    prv = T.cores[(rank - 1) % len(T.cores)]
+    queues = {"v": g.vector, "a": g.scalar, "t": g.tensor, "p": g, "s": g.sync}
+    count = {"v": 0, "a": 0, "t": 0, "p": 0}
+    seen = {q: {} for q in queues}
+    acc = {}
+    psum = set(n for n in SCRATCH if SCRATCH[n][0] == "psum")
+
+    def need(q, regs, write, needs):
+        for (n, lo, hi) in regs:
+            for (qa, sem, val, alo, ahi, aw) in acc.get(n, ()):
+                apart = ahi <= lo or alo >= hi
+                if n in psum and qa != q:
+                    apart = False
+                elif apart or not (aw or write) or (qa == q and write and q == "t"):
+                    continue
+                needs[sem] = max(needs.get(sem, 0), val)
+
+    def note(q, sem, val, regs, write):
+        for (n, lo, hi) in regs:
+            old = acc.get(n, [])
+            if write:
+                old = [a for a in old if not (lo <= a[3] and a[4] <= hi)]
+            acc[n] = old + [(q, sem, val, lo, hi, write)]
+
+    def waits(q, rd, wr):
+        needs = {}
+        need(q, rd, False, needs)
+        need(q, wr, True, needs)
+        for sem in sorted(needs):
+            if seen[q].get(sem, 0) < needs[sem]:
+                queues[q].wait_ge(T.sem[sem], needs[sem])
+                seen[q][sem] = needs[sem]
+
+    def regs(views):
+        return [r for v in views for r in v[1]]
+
+    def op(q, call, rd, wr):
+        rd, wr = regs(rd), regs(wr)
+        waits(q, rd, wr)
+        count[q] += 1
+        call().then_inc(T.sem[q], 1)
+        note(q, q, count[q], rd, False)
+        note(q, q, count[q], wr, True)
+
+    def dma(q, sem, out, in_):
+        waits(q, in_[1], out[1])
+        queues[q].dma_start(out=out[0], in_=in_[0]).then_inc(T.sem[sem], 16)
+        note("d" + sem, sem, 16, in_[1], False)
+        note("d" + sem, sem, 16, out[1], True)
+
+    sent = [0]
+
+    def send(dst_name, src_name, lo, hi, sem):
+        src, dst = V(src_name, lo, hi), V(dst_name, lo, hi)
+        waits("p", src[1], [])
+        rid, pid, _ = topo.addr(nxt)
+        g.remote_dma(out_ap=dst[0], in_ap=src[0], remote_sem=T.sem[sem], local_sem=T.sem["loc"],
+                     pid=pid, routing_id=rid, dma_engine_mask=topo.mask(core, nxt))
+        sent[0] += len(topo.engines(core, nxt))
+        note("r", sem, len(topo.engines(prv, core)), dst[1], True)
+
+    def V(name, lo, hi, st=1):
+        if name in PIECE:
+            name, base = PIECE[name]
+            lo, hi = lo + base, hi + base
+        return (T[name][:, lo:hi] if st == 1 else T[name][:, lo:hi:st], [(name, lo, hi)])
+
+    def ALL(name):
+        return (T[name][:], [(name, 0, SCRATCH[name][1][1] if name in SCRATCH else 1)])
+
+    def IND(win, off):
+        return (win[0].indirect(off[0]), win[1] + off[1])
+
+    def cols(*vs):
+        return [v for v in vs if not isinstance(v, (int, float)) and v is not None]
+
+    def raw(v):
+        return v if isinstance(v, (int, float)) or v is None else v[0]
+
+    def tt(o, a, b, f):
+        op("v", lambda: g.vector.tensor_tensor(out=o[0], in0=a[0], in1=b[0], op=f), [a, b], [o])
+
+    def ts(o, a, s1, f1, s2=None, f2=None):
+        if f2 is None:
+            op("v", lambda: g.vector.tensor_scalar(out=o[0], in0=a[0], scalar1=raw(s1), scalar2=None, op0=f1), [a] + cols(s1), [o])
+        else:
+            op("v", lambda: g.vector.tensor_scalar(out=o[0], in0=a[0], scalar1=raw(s1), scalar2=raw(s2), op0=f1, op1=f2),
+               [a] + cols(s1, s2), [o])
+
+    def cp(o, a):
+        op("v", lambda: g.vector.tensor_copy(out=o[0], in_=a[0]), [a], [o])
+
+    def scan(o, d0, d1, f0, f1):
+        op("v", lambda: g.vector.tensor_tensor_scan(out=o[0], data0=d0[0], data1=d1[0], initial=0.0, op0=f0, op1=f1), [d0, d1], [o])
+
+    def fill(o, c):
+        op("v", lambda: g.vector.memset(o[0], c), [], [o])
+
+    def act(o, a, f=ACT.Copy):
+        op("a", lambda: g.scalar.activation(out=o[0], in_=a[0], func=f), [a], [o])
+
+    def line(o, a, scale, bias):
+        op("a", lambda: g.scalar.activation(out=o[0], in_=a[0], func=ACT.Identity, bias=raw(bias), scale=scale), [a] + cols(bias), [o])
+
+    def mm(o, l, r, start=True, stop=True):
+        op("t", lambda: g.tensor.matmul(out=o[0], lhsT=l[0], rhs=r[0], start=start, stop=stop), [l, r], [o])
+
+    def iota(o, pattern, base, cm):
+        op("p", lambda: g.iota(o[0], pattern, base, cm, allow_small_or_imprecise_dtypes=True), [], [o])
+
+    def select(o, a, pattern, f, base, cm):
+        op("p", lambda: g.affine_select(o[0], a[0], pattern, f, 0.0, base, cm), [a], [o])
+
+    XR, PR = V("XW", 0, 4112), V("PW", 0, 4112)
+    XA, PA = V("XW", 0, PADW), V("PW", 0, PADW)
+
+    def tile0(name, src):
+        t = T[name]
+        act((t[:, :, 0:16], [(name, 0, 16)]), V(src, 0, 64))
+        for w in (16, 32, 64):
+            act((t[:, :, w:2 * w], [(name, w, 2 * w)]), (t[:, :, 0:w], [(name, 0, w)]))
+
+    def tile1(name):
+        t = T[name]
+        act((t[:, :, 128:256], [(name, 128, 256)]), (t[:, :, 0:128], [(name, 0, 128)]))
+
+    def pgather(s, half):
+        return V("PG", 1024 * half, 1024 * half + 1024), IND(PR, V("OU%d" % s, 64 * half, 64 * half + 64))
+
+    def reduce16(src, c0, c1, w, bank, first=None):
+        out = V(bank, 0, c1 - c0)
+        if first is not None:
+            mm(out, first[0], first[1], True, False)
+        for i in range(16):
+            mm(out, V(w, 128 * i, 128 * i + 128), (T[src][:, 16 * c0 + i:16 * c1:16], [(src, 16 * c0, 16 * c1)]),
+               first is None and i == 0, i == 15)
+
+    def gather_abs(L, j, off, tname):
+        lo = 512 * L + TW * j
+        tt(V("DF", lo, lo + TW), IND(XR, V(off, lo // 16, (lo + TW) // 16)), (T[tname][:, L, 0:TW], [(tname, 0, TW)]), ALU.subtract)
+        act(V("AB", lo, lo + TW), V("DF", lo, lo + TW), ACT.Abs)
+
+    def h_of(piece, s):
+        a, b, bank, sem = HP[piece]
+        u = V(bank, 0, b - a)
+        tt(V("hm", a, b), u, V("OQ%d" % (s % 2), a, b), ALU.mult)
+        tt(V("pS", 256 + a, 256 + b), u, V("Q32", a, b), ALU.add)
+        tt(V("hv", a, b), V("pS", 256 + a, 256 + b), V("hm", a, b), ALU.add)
+        ts(V("hs", a, b), V("hv", a, b), 5, ALU.arith_shift_right, 4095, ALU.bitwise_and)
+        ts(V("HS%d" % s, a, b), V("hs", a, b), 1.0, ALU.add)
+        send("HR%d" % s, "HS%d" % s, a, b, "%s%d" % (sem, s))
+
+    dma("s", "d_px", V("pxi", 0, 256), ALL("px"))
+    dma("a", "d_ol", V("oli", 0, 128), ALL("ol"))
+    dma("s", "d_z", V("ZS0", 0, 64), ALL("z"))
+    dma("a", "d_tl", V("tli", 0, 128), ALL("tl"))
+    fill(V("ones", 0, 128), 1.0)
+    fill(V("XW", 0, 16), 0.0)
+    fill(V("XW", 4096, PADW), 0.0)
+    dma("s", "d_x", V("XW", 1, 4097), ALL("x"))
+    dma("a", "d_nl", V("nli", 0, 128), ALL("nl"))
+    dma("a", "d_th", ALL("thi"), ALL("th"))
+    iota(V("pidx", 0, 1), [[0, 1]], 0, 1)
+    select(V("G1", 0, 128), V("ones", 0, 128), [[-16, 8], [0, 16]], ALU.is_ge, 0, 1)
+    select(V("GM", 0, 128), V("G1", 0, 128), [[16, 8], [0, 16]], ALU.is_ge, 15, -1)
+    iota(V("W", 0, 2048), [[0, 2048]], 0, 0)
+    fill(V("PW", 0, PADW), 0.0)
+    ts(V("pxt", 0, 256), V("pxi", 0, 256), 1, ALU.add)
+    ts(V("pxt", 256, 512), V("pxt", 0, 256), 6, ALU.arith_shift_right)
+    cp(V("LH", 256, 512), V("pxt", 256, 512))
+    waits("a", [("LH", 256, 512), ("PW", 0, PADW)], [])
+    g.scalar.dma_start(out=T["PW"][1:128:16, 1:4097], in_=T["LH"][:, 256:512]).then_inc(T.sem["d_hi"], 16)
+    ts(V("pxt", 0, 256), V("pxt", 0, 256), 63, ALU.bitwise_and)
+    cp(V("LH", 0, 256), V("pxt", 0, 256))
+    dma("s", "d_lo", (T["PW"][0:128:16, 1:4097], [("PW", 1, 4097)]), V("LH", 0, 256))
+    note("dd_hi", "d_hi", 16, [("LH", 256, 512)], False)
+    acc["PW"] = acc["PW"] + [("dd_hi", "d_hi", 16, 1, 4097, True)]
+    for L in range(4):
+        ts(V("OW0", 32 * L, 32 * L + 32), V("oli", L, 128, 4), 1, ALU.add)
+    cp(V("OU0", 0, 128), V("OW0", 0, 128))
+    fill(V("WP", 0, 2048), 0.0)
+    ts(V("p16i", 0, 1), V("pidx", 0, 1), 15, ALU.bitwise_and)
+    cp(V("p16", 0, 1), V("p16i", 0, 1))
+    ts(V("q0", 0, 1), V("p16", 0, 1), 0.0, ALU.is_equal)
+    ts(V("q1", 0, 1), V("p16", 0, 1), 1.0, ALU.is_equal)
+    ts(V("wp1", 0, 1), V("q1", 0, 1), 64.0, ALU.mult)
+    ts(V("be1", 0, 1), V("q0", 0, 1), -64.0, ALU.mult)
+    tt(V("wp", 0, 1), V("wp1", 0, 1), V("q0", 0, 1), ALU.add)
+    tt(V("beta", 0, 1), V("be1", 0, 1), V("q1", 0, 1), ALU.add)
+    ts(V("GP", 0, 8), V("GM", 0, 128, 16), V("wp", 0, 1), ALU.mult)
+    ts(V("GA", 0, 8), V("GM", 0, 128, 16), 32.0, ALU.mult)
+    for i in range(16):
+        cp(V("WP", 128 * i + i, 128 * i + 128, 16), V("GP", 0, 8))
+    tile0("ztb", "ZS0")
+    tile1("ztb")
+    act(*pgather(0, 0))
+    cp(*pgather(0, 1))
+    for i in range(16):
+        act(V("W", 128 * i + i, 128 * i + 128, 16), V("GA", 0, 8))
+    for L in range(4):
+        cp(V("ZS0", 64 + 32 * L, 96 + 32 * L), V("tli", L, 128, 4))
+    for L in range(4):
+        ts(V("NS0", 32 * L, 32 * L + 32), V("nli", L, 128, 4), 1, ALU.add)
+    ts(V("MB", 0, 128), V("ZS0", 64, 192), 0.0, ALU.is_gt)
+    ts(V("pS", 384, 512), V("ZS0", 64, 192), 0.0, ALU.is_le)
+    tt(V("NM", 0, 128), V("pS", 384, 512), V("NS0", 0, 128), ALU.mult)
+    select(V("LT", 0, 128), V("GM", 0, 128), [[1, 128]], ALU.is_gt, 0, -1)
+    iota(V("mod16", 0, 192), [[0, 12], [1, 16]], 0, 0)
+    iota(V("colc", 0, 128), [[1, 128]], 0, 0)
+    iota(V("mod32", 0, 128), [[0, 4], [1, 32]], 0, 0)
+    iota(V("dump0", 0, 4), [[16, 4]], DUMP0, 0)
+    select(ALL("GE1"), (T["ones"][0:8, 0:128], [("ones", 0, 128)]), [[1, 128]], ALU.is_ge, 0, -16)
+    select(ALL("GE"), ALL("GE1"), [[-1, 128]], ALU.is_ge, 15, 16)
+
+    def late_constants():
+        fill(ALL("oneb"), 1.0)
+        ts(ALL("CQ"), (T["colc"][0:1, 0:128], [("colc", 0, 128)]), -0.25, ALU.mult, 31.75, ALU.add)
+        ts(V("C2", 0, 128), V("colc", 0, 128), -0.5, ALU.mult, 130560.0 + 63.5, ALU.add)
+        ts(V("SEG16", 0, 192), V("mod16", 0, 192), 0.0, ALU.is_gt)
+        ts(V("SEG32", 0, 128), V("mod32", 0, 128), 0.0, ALU.is_gt)
+        ts(V("DM", 0, 128), V("mod16", 0, 128), V("p16", 0, 1), ALU.is_equal)
+        ts(V("dump", 0, 4), V("dump0", 0, 4), V("p16", 0, 1), ALU.add)
+        fill(V("GL", 0, 128), 0.0)
+        cp(V("GL", 0, 128, 16), V("GM", 0, 128, 16))
+        cp(ALL("thf"), ALL("thi"))
+        mm(V("pM", 128, 133), ALL("GE"), ALL("thf"))
+        ts(V("LM", 0, 5), V("pM", 128, 133), 32.0, ALU.mult, 31.75, ALU.add)
+        fill(V("OW0", 128, 256), 0.0)
+        fill(V("OW1", 128, 256), 0.0)
+
+    for s in range(S):
+        par, nxp = s % 2, (s + 1) % 2
+        last = s == S - 1
+        zr, nr, hr, zs1 = "ZR%d" % s, "NR%d" % s, "HR%d" % s, "ZS%d" % (s + 1)
+        send("OU%d" % (s + 1), "OU%d" % s, 0, 128, "rO%d" % s)
+        send(zr, "ZS%d" % s, 0, 192, "rZ%d" % s)
+        reduce16("PG", 0, 64, "WP", PB[0])
+        if s > 0:
+            mm(V("pM", 136, 137), V("GM", 0, 128), V("rs", 0, 1))
+            line(V("A32", 0, 1), V("pM", 136, 137), 32.0, -8388608.0 - 1184.0)
+            line(V("Q32", 0, 128), V("OW%d" % par, 0, 128), 1184.0, V("A32", 0, 1))
+        else:
+            line(V("OQ0", 0, 128), V("OW0", 0, 128), 1.0 / 32, -1.0 / 32)
+            line(V("Q32", 0, 128), V("OW0", 0, 128), 1184.0, -8388608.0 - 1184.0)
+        reduce16("PG", 64, 128, "WP", PB[1])
+
+        def road(half):
+            a, b = 64 * half, 64 * half + 64
+            tt(V("pS", 384 + a, 384 + b), V(PB[half], 0, 64), V("MB", a, b), ALU.mult)
+            tt(V("R1", a, b), V("pS", 384 + a, 384 + b), V("NM", a, b), ALU.add)
+            cp(V("RU", a, b), V("R1", a, b))
+
+        road(0)
+        for L in (0, 1):
+            for j in (0, 1):
+                gather_abs(L, j, "RU", "ztb")
+        reduce16("AB", 0, 64, "W", "pUA")
+        road(1)
+        for j in (0, 1):
+            gather_abs(2, j, "RU", "ztb")
+        reduce16("AB", 64, 96, "W", "pUB")
+        gather_abs(3, 0, "RU", "ztb")
+        h_of(0, s)
+        gather_abs(3, 1, "RU", "ztb")
+        reduce16("AB", 96, 128, "W", "pUC")
+        h_of(1, s)
+        if s > 0:
+            tt(V("pS", 128, 256), V("pS", 0, 128), V("hN", 0, 128), ALU.mult)
+            tt(V("NS%d" % s, 0, 128), V("pS", 128, 256), V("NR%d" % (s - 1), 0, 128), ALU.add)
+        date = V(zr, 64, 192)
+        tile0("ztc", zr)
+        tile1("ztc")
+
+        def known():
+            cp(V("OW%d" % nxp, 0, 128), V("OU%d" % (s + 1), 0, 128))
+            ts(V("e1", 0, 128), date, float(s), ALU.is_gt, -BIG, ALU.mult)
+            ts(V("e2", 0, 128), date, 99.0, ALU.is_lt)
+
+        if s > 0:
+            known()
+        h_of(2, s)
+        send(nr, "NS%d" % s, 0, 128, "rN%d" % s)
+        if s == 0:
+            late_constants()
+            known()
+        tt(V("RT0", 0, 128), V("e1", 0, 128), V("e2", 0, 128), ALU.mult)
+        ts(V("RT", 0, 128), V("RT0", 0, 128), V("LM", s, s + 1), ALU.add)
+        if last:
+            dma("s", "o_lo", V("LO", 0, 256), (T["PW"][0:128:16, 1:4097], [("PW", 1, 4097)]))
+            dma("s", "o_hi", V("LO", 256, 512), (T["PW"][1:128:16, 1:4097], [("PW", 1, 4097)]))
+        line(V("OQ%d" % nxp, 0, 128), V("OW%d" % nxp, 0, 128), 1.0 / 32, -1.0 / 32)
+        line(V("ST", 0, 128), date, -1.0, float(s + 2))
+        for half in (0, 1):
+            a, b = 64 * half, 64 * half + 64
+            for L in (2 * half, 2 * half + 1):
+                for j in (0, 1):
+                    gather_abs(L, j, hr, "ztc")
+            if last and half == 0:
+                line(V("pR", 256, 512), V("LO", 256, 512), 64.0, -1.0)
+            reduce16("AB", a, b, "W", KB[half], (ALL("oneb"), (T["CQ"][:, a:b], [("CQ", a, b)])))
+        cp(V("HW", 0, 128), V(hr, 0, 128))
+
+        def keys(half):
+            a, b = 64 * half, 64 * half + 64
+            kd = V(KB[half], 0, 64)
+            tt(V("K2", a, b), V("C2", a, b), kd, ALU.subtract)
+            scan(V("SM", a, b), V("SEG32", a, b), kd, ALU.mult, ALU.max)
+            scan(V("SM", 128 + a, 128 + b), V("SEG32", a, b), V("K2", a, b), ALU.mult, ALU.max)
+
+        def redeem(half):
+            a, b = 64 * half, 64 * half + 64
+            tt(V("pS", a, b), V(KB[half], 0, 64), V("RT", a, b), ALU.is_le)
+            tt(V("pS", 128 + a, 128 + b), V("pS", a, b), V("ST", a, b), ALU.mult)
+            tt(V("pS", 256 + a, 256 + b), V("pS", 128 + a, 128 + b), V(zr, 64 + a, 64 + b), ALU.add)
+
+        if last:
+            tt(V("YPg", 0, 256), V("pR", 256, 512), V("LO", 0, 256), ALU.add)
+            dma("s", "o_pf", (T["PF"][0:128:16, 1:4097], [("PF", 1, 4097)]), V("YPg", 0, 256))
+        keys(0)
+        redeem(0)
+        tt(V("hN", 0, 128), V("HW", 0, 128), V(nr, 0, 128), ALU.subtract)
+        keys(1)
+        lastk = V("SM", 31, 128, 32)
+        ts(V("KI", 0, 8), V("SM", 31, 256, 32), 4.0, ALU.mult)
+        ts(V("nogo", 0, 4), lastk, V("LM", s, s + 1), ALU.is_le, 128.0, ALU.mult)
+        ts(V("CI", 0, 8), V("KI", 0, 8), 127, ALU.bitwise_and)
+        tt(V("CI", 8, 12), V("CI", 0, 4), V("nogo", 0, 4), ALU.subtract)
+        ts(V("OFF", 0, 12), V("CI", 0, 12), -1.0, ALU.mult, 127.0, ALU.add)
+        tt(V("GD", 0, 128), IND(V("HW", 0, 128), V("OFF", 0, 8)), V("DM", 0, 128), ALU.mult)
+        tt(V("GD", 128, 192), IND(V("OW%d" % nxp, 0, 256), V("OFF", 8, 12)), V("DM", 0, 64), ALU.mult)
+        mm(V("pR", 0, 64), V("LT", 0, 128), V("GD", 128, 192))
+        mm(V("pR", 64, 128), V("GM", 0, 128), V("GD", 0, 64))
+        if not last:
+            mm(V("pR", 128, 192), V("GL", 0, 128), V("GD", 0, 64))
+        mm(V("pM", 0, 64), V("LT", 0, 128), V("GD", 64, 128))
+        scan(V("OWN", 64, 192), V("SEG16", 0, 128), V("GD", 64, 192), ALU.mult, ALU.add)
+        cp(V("HB", 0, 4), V("OWN", 79, 128, 16))
+        tt(V("gz", 0, 64), IND(XR, V("HB", 0, 4)), V(zr, 0, 64), ALU.add)
+        ts(V("zi", 0, 64), V("gz", 0, 64), 0.5, ALU.mult, -0.25, ALU.add)
+        cp(V(zs1, 0, 64), V("zi", 0, 64))
+
+        def resolve(e, f, fin, fu, bank, own):
+            for L in range(4):
+                ts(V(e, 16 * L, 16 * L + 16), V(bank, 16 * L, 16 * L + 16), V("OWN", own + 16 * L + 15, own + 16 * L + 16),
+                   ALU.is_equal, V("dump", L, L + 1), ALU.mult)
+            scan(V(f, 0, 64), V("SEG16", 0, 64), V(e, 0, 64), ALU.mult, ALU.max)
+            tt(V(fin, 0, 4), V(f, 15, 64, 16), V("OWN", own + 15, own + 64, 16), ALU.max)
+            cp(V(fu, 0, 8, 2), V(fin, 0, 4))
+
+        def write(win, fu, data):
+            for L in (3, 2, 1, 0):
+                cp(IND(win, V(fu, 2 * L, 2 * L + 1)), V(data, 16 * L, 16 * L + 16))
+
+        def items():
+            resolve("EX", "FX", "fx", "fxu", "pM", 64)
+            write(XA, "fxu", "zi")
+
+        def dates():
+            redeem(1)
+            tt(V("gk", 0, 4), lastk, V("nogo", 0, 4), ALU.subtract)
+            for L in range(4):
+                ts(V("RF", 32 * L, 32 * L + 32), V(KB[L // 2], 32 * (L % 2), 32 * (L % 2) + 32), V("gk", L, L + 1),
+                   ALU.is_equal, 99.0, ALU.mult)
+            tt(V(zs1, 64, 192), V("pS", 256, 384), V("RF", 0, 128), ALU.max)
+
+        if not last:
+            tile0("ztb", zs1)
+            ts(V("hi", 0, 64), V("pR", 64, 128), -31.5, ALU.add, 1.0 / 64, ALU.mult)
+            resolve("EP", "FP", "fp", "fpu", "pR", 128)
+            ts(V("ht", 0, 64), V("hi", 0, 64), V("beta", 0, 1), ALU.mult)
+            tt(V("PD", 0, 64), V("pR", 128, 192), V("ht", 0, 64), ALU.add)
+            write(PA, "fpu", "PD")
+            act(*pgather(s + 1, 0))
+            tile1("ztb")
+            act(*pgather(s + 1, 1))
+            dates()
+            op("v", lambda: g.vector.tensor_reduce(out=T["rs"][:, 0:1], in_=T["pS"][:, 0:128], axis=AxisListType.X, op=ALU.add),
+               [V("pS", 0, 128)], [V("rs", 0, 1)])
+            ts(V("MB", 0, 128), V(zs1, 64, 192), float(s + 1), ALU.is_gt)
+            ts(V("pS", 384, 512), V(zs1, 64, 192), float(s + 1), ALU.is_le)
+            tt(V("NM", 0, 128), V("pS", 384, 512), V(nr, 0, 128), ALU.mult)
+            items()
+        else:
+            dma("a", "o_z", ALL("yz"), V(zs1, 0, 64))
+            items()
+            dma("s", "o_x", ALL("yx"), V("XW", 1, 4097))
+            resolve("EP", "FP", "fp", "fpu", "pR", 128)
+            ts(V("ht", 0, 64), V("pR", 64, 128), -1.0, ALU.add)
+            write(V("PF", 0, PADW), "fpu", "ht")
+            dma("a", "o_p", ALL("yp"), (T["PF"][0:128:16, 1:4097], [("PF", 1, 4097)]))
+            dates()
+            for L in range(4):
+                cp(V("YT", L, 128, 4), V(zs1, 64 + 32 * L, 96 + 32 * L))
+            dma("a", "o_t", ALL("yt"), V("YT", 0, 128))
+            tt(V("pS", 128, 256), V("pS", 0, 128), V("hN", 0, 128), ALU.mult)
+            tt(V("NS%d" % (s + 1), 0, 128), V("pS", 128, 256), V(nr, 0, 128), ALU.add)
+            for L in range(4):
+                ts(V("YN", L, 128, 4), V("NS%d" % (s + 1), 32 * L, 32 * L + 32), -1.0, ALU.add)
+            dma("a", "o_n", ALL("yn"), V("YN", 0, 128))
+    for q in ("v", "a", "t", "p"):
+        g.wait_ge(T.sem[q], count[q])
+    g.wait_ge(T.sem["loc"], sent[0])
+    for n in DMAS:
+        g.wait_ge(T.sem[n], 16)
+    for s in range(S):
+        for k in RECV:
+            g.wait_ge(T.sem["%s%d" % (k, s)], len(topo.engines(prv, core)))

@@ -13,23 +13,22 @@ SCRATCH = {
     "ztb": ("sbuf", [128, 4, TW], "bfloat16"), "ztc": ("sbuf", [128, 4, TW], "bfloat16"),
     "DF": _sb(2048, "bfloat16"), "AB": _sb(2048, "bfloat16"), "PG": _sb(2048, "bfloat16"),
     "W": _sb(2048, "bfloat16"), "WP": _sb(2048, "bfloat16"),
-    "pxi": _sb(256, "int32"), "pxt": _sb(512, "int32"), "LH": _sb(512, "bfloat16"),
+    "pxi": _sb(256, "int32"), "pxt": _sb(256, "int32"), "LH": _sb(512, "bfloat16"),
     "oli": _sb(128, "int32"), "nli": _sb(128, "int32"), "tli": _sb(128, "int32"),
     "thi": _sb(5, "int32", 8), "thf": _sb(5, "float32", 8), "GE1": _sb(128, "float32", 8), "GE": _sb(128, "float32", 8),
-    "ones": _sb(128), "oneb": _sb(128, "bfloat16", 1), "CQ": _sb(128, "bfloat16", 1),
-    "G1": _sb(128), "GM": _sb(128), "GL": _sb(128), "LT": _sb(128), "GA": _sb(8), "GP": _sb(8),
-    "mod16": _sb(192), "mod32": _sb(128), "colc": _sb(128), "C2": _sb(128), "SEG16": _sb(192), "SEG32": _sb(128), "DM": _sb(128),
-    "pidx": _sb(1, "int32"), "p16i": _sb(1, "int32"), "p16": _sb(1), "q0": _sb(1), "q1": _sb(1), "wp1": _sb(1), "be1": _sb(1),
-    "beta": _sb(1), "wp": _sb(1), "dump0": _sb(4), "dump": _sb(4), "LM": _sb(5),
+    "ones": _sb(128), "neg": _sb(128), "oneb": _sb(128, "bfloat16", 1), "CQ": _sb(128, "bfloat16", 1),
+    "one2": _sb(192), "G1": _sb(128), "GM": _sb(128), "NI": _sb(128), "LT": _sb(128), "GA": _sb(8), "GP": _sb(8),
+    "mod16": _sb(128), "colc": _sb(128), "C2": _sb(128), "SEG16": _sb(128), "SEG32": _sb(128), "DM": _sb(128), "ND": _sb(144),
+    "pidx": _sb(1, "int32"), "p16i": _sb(1, "int32"), "p16": _sb(1), "q0": _sb(1), "q1": _sb(1), "wp": _sb(1),
+    "dump0": _sb(8), "dump": _sb(8), "dumpw": _sb(128), "LM": _sb(5),
     "OW0": _sb(256), "OW1": _sb(256), "OQ0": _sb(128), "OQ1": _sb(128), "HW": _sb(128), "Q32": _sb(128), "A32": _sb(1), "rs": _sb(1),
-    "MB": _sb(128), "NM": _sb(128), "R1": _sb(128), "RU": _sb(128, "uint16"),
+    "MB": _sb(128), "R1": _sb(128), "RU": _sb(128, "uint16"),
     "hm": _sb(128), "hv": _sb(128, "int32"), "hs": _sb(128, "int32"),
     "e1": _sb(128), "e2": _sb(128), "RT0": _sb(128), "RT": _sb(128), "ST": _sb(128), "hN": _sb(128), "K2": _sb(128), "SM": _sb(256),
     "KI": _sb(8, "int32"), "CI": _sb(12, "int32"), "nogo": _sb(4, "int32"), "gk": _sb(4), "OFF": _sb(12, "uint16"),
-    "GD": _sb(192), "OWN": _sb(192), "HB": _sb(4, "uint16"), "gz": _sb(64), "zi": _sb(64, "int32"),
-    "EP": _sb(64), "FP": _sb(64), "fp": _sb(4), "fpu": _sb(8, "uint16"),
-    "EX": _sb(64), "FX": _sb(64), "fx": _sb(4), "fxu": _sb(8, "uint16"),
-    "hi": _sb(64, "int32"), "ht": _sb(64), "PD": _sb(64, "bfloat16"), "RF": _sb(128),
+    "GD": _sb(208), "OWN": _sb(144), "HB": _sb(4, "uint16"), "gz": _sb(64), "zi": _sb(64, "int32"),
+    "E": _sb(128), "F": _sb(128), "f1": _sb(8), "f2": _sb(8), "fu": _sb(16, "uint16"),
+    "hx": _sb(64, "bfloat16"), "ht": _sb(64), "PD": _sb(64, "bfloat16"), "RF": _sb(128),
     "YN": _sb(128), "YT": _sb(128), "YPg": _sb(256), "LO": _sb(512, "bfloat16"),
     "ZR": _sb(192 * S, "bfloat16"),
     "NR": _sb(128 * S),
@@ -50,6 +49,7 @@ SEMAPHORES = ["v", "a", "t", "p", "loc"] + ["%s%d" % (k, s) for s in range(S) fo
 HP = ((0, 64, "pUA", "rA"), (64, 96, "pUB", "rB"), (96, 128, "pUC", "rC"))
 KB = ("pUA", "pUB")
 PB = ("pPA", "pPB")
+A0 = -8388608.0 - 1184.0
 
 
 def rank_program(g, core, T, topo):
@@ -173,20 +173,20 @@ def rank_program(g, core, T, topo):
     XR, PR = V("XW", 0, 4112), V("PW", 0, 4112)
     XA, PA = V("XW", 0, PADW), V("PW", 0, PADW)
 
-    def tile0(name, src):
+    def tile(name, src):
         t = T[name]
         act((t[:, :, 0:16], [(name, 0, 16)]), V(src, 0, 64))
         for w in (16, 32, 64):
             act((t[:, :, w:2 * w], [(name, w, 2 * w)]), (t[:, :, 0:w], [(name, 0, w)]))
 
-    def tile1(name):
+    def tile_end(name):
         t = T[name]
         act((t[:, :, 128:256], [(name, 128, 256)]), (t[:, :, 0:128], [(name, 0, 128)]))
 
-    def pgather(s, half):
-        return V("PG", 1024 * half, 1024 * half + 1024), IND(PR, V("OU%d" % s, 64 * half, 64 * half + 64))
+    def pgather(s, a, b):
+        return V("PG", 16 * a, 16 * b), IND(PR, V("OU%d" % s, a, b))
 
-    def reduce16(src, c0, c1, w, bank, first=None):
+    def reduce16(src, c0, c1, w, bank, first):
         out = V(bank, 0, c1 - c0)
         if first is not None:
             mm(out, first[0], first[1], True, False)
@@ -212,25 +212,25 @@ def rank_program(g, core, T, topo):
     dma("s", "d_px", V("pxi", 0, 256), ALL("px"))
     dma("a", "d_ol", V("oli", 0, 128), ALL("ol"))
     dma("s", "d_z", V("ZS0", 0, 64), ALL("z"))
-    dma("a", "d_tl", V("tli", 0, 128), ALL("tl"))
+    dma("a", "d_nl", V("nli", 0, 128), ALL("nl"))
     fill(V("ones", 0, 128), 1.0)
     fill(V("XW", 0, 16), 0.0)
     fill(V("XW", 4096, PADW), 0.0)
     dma("s", "d_x", V("XW", 1, 4097), ALL("x"))
-    dma("a", "d_nl", V("nli", 0, 128), ALL("nl"))
+    dma("a", "d_tl", V("tli", 0, 128), ALL("tl"))
     dma("a", "d_th", ALL("thi"), ALL("th"))
+    fill(V("neg", 0, 128), -1.0)
     iota(V("pidx", 0, 1), [[0, 1]], 0, 1)
     select(V("G1", 0, 128), V("ones", 0, 128), [[-16, 8], [0, 16]], ALU.is_ge, 0, 1)
     select(V("GM", 0, 128), V("G1", 0, 128), [[16, 8], [0, 16]], ALU.is_ge, 15, -1)
+    select(V("NI", 0, 128), V("neg", 0, 128), [[1, 128]], ALU.is_equal, 0, -1)
     iota(V("W", 0, 2048), [[0, 2048]], 0, 0)
     fill(V("PW", 0, PADW), 0.0)
-    ts(V("pxt", 0, 256), V("pxi", 0, 256), 1, ALU.add)
-    ts(V("pxt", 256, 512), V("pxt", 0, 256), 6, ALU.arith_shift_right)
-    cp(V("LH", 256, 512), V("pxt", 256, 512))
+    ts(V("LH", 256, 512), V("pxi", 0, 256), 1, ALU.add)
     waits("a", [("LH", 256, 512), ("PW", 0, PADW)], [])
     g.scalar.dma_start(out=T["PW"][1:128:16, 1:4097], in_=T["LH"][:, 256:512]).then_inc(T.sem["d_hi"], 16)
-    ts(V("pxt", 0, 256), V("pxt", 0, 256), 63, ALU.bitwise_and)
-    cp(V("LH", 0, 256), V("pxt", 0, 256))
+    ts(V("pxt", 0, 256), V("pxi", 0, 256), 1, ALU.add)
+    tt(V("LH", 0, 256), V("pxt", 0, 256), V("LH", 256, 512), ALU.subtract)
     dma("s", "d_lo", (T["PW"][0:128:16, 1:4097], [("PW", 1, 4097)]), V("LH", 0, 256))
     note("dd_hi", "d_hi", 16, [("LH", 256, 512)], False)
     acc["PW"] = acc["PW"] + [("dd_hi", "d_hi", 16, 1, 4097, True)]
@@ -239,96 +239,100 @@ def rank_program(g, core, T, topo):
     cp(V("OU0", 0, 128), V("OW0", 0, 128))
     fill(V("WP", 0, 2048), 0.0)
     ts(V("p16i", 0, 1), V("pidx", 0, 1), 15, ALU.bitwise_and)
-    cp(V("p16", 0, 1), V("p16i", 0, 1))
-    ts(V("q0", 0, 1), V("p16", 0, 1), 0.0, ALU.is_equal)
-    ts(V("q1", 0, 1), V("p16", 0, 1), 1.0, ALU.is_equal)
-    ts(V("wp1", 0, 1), V("q1", 0, 1), 64.0, ALU.mult)
-    ts(V("be1", 0, 1), V("q0", 0, 1), -64.0, ALU.mult)
-    tt(V("wp", 0, 1), V("wp1", 0, 1), V("q0", 0, 1), ALU.add)
-    tt(V("beta", 0, 1), V("be1", 0, 1), V("q1", 0, 1), ALU.add)
-    ts(V("GP", 0, 8), V("GM", 0, 128, 16), V("wp", 0, 1), ALU.mult)
-    ts(V("GA", 0, 8), V("GM", 0, 128, 16), 32.0, ALU.mult)
-    for i in range(16):
-        cp(V("WP", 128 * i + i, 128 * i + 128, 16), V("GP", 0, 8))
-    tile0("ztb", "ZS0")
-    tile1("ztb")
-    act(*pgather(0, 0))
-    cp(*pgather(0, 1))
-    for i in range(16):
-        act(V("W", 128 * i + i, 128 * i + 128, 16), V("GA", 0, 8))
-    for L in range(4):
-        cp(V("ZS0", 64 + 32 * L, 96 + 32 * L), V("tli", L, 128, 4))
     for L in range(4):
         ts(V("NS0", 32 * L, 32 * L + 32), V("nli", L, 128, 4), 1, ALU.add)
+    cp(V("p16", 0, 1), V("p16i", 0, 1))
+    ts(V("GA", 0, 8), V("GM", 0, 128, 16), 32.0, ALU.mult)
+    ts(V("q0", 0, 1), V("p16", 0, 1), 0.0, ALU.is_equal)
+    ts(V("q1", 0, 1), V("p16", 0, 1), 1.0, ALU.is_equal)
+    tt(V("wp", 0, 1), V("q1", 0, 1), V("q0", 0, 1), ALU.add)
+    ts(V("GP", 0, 8), V("GM", 0, 128, 16), V("wp", 0, 1), ALU.mult)
+    for i in range(16):
+        cp(V("WP", 128 * i + i, 128 * i + 128, 16), V("GP", 0, 8))
+    tile("ztb", "ZS0")
+    tile_end("ztb")
+    act(*pgather(0, 0, 64))
+    for L in range(4):
+        cp(V("ZS0", 64 + 32 * L, 96 + 32 * L), V("tli", L, 128, 4))
+    cp(*pgather(0, 64, 128))
     ts(V("MB", 0, 128), V("ZS0", 64, 192), 0.0, ALU.is_gt)
-    ts(V("pS", 384, 512), V("ZS0", 64, 192), 0.0, ALU.is_le)
-    tt(V("NM", 0, 128), V("pS", 384, 512), V("NS0", 0, 128), ALU.mult)
+    for i in range(16):
+        act(V("W", 128 * i + i, 128 * i + 128, 16), V("GA", 0, 8))
     select(V("LT", 0, 128), V("GM", 0, 128), [[1, 128]], ALU.is_gt, 0, -1)
-    iota(V("mod16", 0, 192), [[0, 12], [1, 16]], 0, 0)
+    iota(V("mod16", 0, 128), [[0, 8], [1, 16]], 0, 0)
     iota(V("colc", 0, 128), [[1, 128]], 0, 0)
-    iota(V("mod32", 0, 128), [[0, 4], [1, 32]], 0, 0)
-    iota(V("dump0", 0, 4), [[16, 4]], DUMP0, 0)
+    iota(V("dump0", 0, 8), [[0, 2], [16, 4]], DUMP0, 0)
+    iota(V("dumpw", 0, 128), [[16, 4], [0, 32]], DUMP0, 0)
+    select(V("SEG16", 0, 128), V("ones", 0, 128), [[0, 8], [1, 16]], ALU.is_gt, 0, 0)
+    select(V("SEG32", 0, 128), V("ones", 0, 128), [[0, 4], [1, 32]], ALU.is_gt, 0, 0)
     select(ALL("GE1"), (T["ones"][0:8, 0:128], [("ones", 0, 128)]), [[1, 128]], ALU.is_ge, 0, -16)
     select(ALL("GE"), ALL("GE1"), [[-1, 128]], ALU.is_ge, 15, 16)
 
     def late_constants():
-        fill(ALL("oneb"), 1.0)
-        ts(ALL("CQ"), (T["colc"][0:1, 0:128], [("colc", 0, 128)]), -0.25, ALU.mult, 31.75, ALU.add)
-        ts(V("C2", 0, 128), V("colc", 0, 128), -0.5, ALU.mult, 130560.0 + 63.5, ALU.add)
-        ts(V("SEG16", 0, 192), V("mod16", 0, 192), 0.0, ALU.is_gt)
-        ts(V("SEG32", 0, 128), V("mod32", 0, 128), 0.0, ALU.is_gt)
-        ts(V("DM", 0, 128), V("mod16", 0, 128), V("p16", 0, 1), ALU.is_equal)
-        ts(V("dump", 0, 4), V("dump0", 0, 4), V("p16", 0, 1), ALU.add)
-        fill(V("GL", 0, 128), 0.0)
-        cp(V("GL", 0, 128, 16), V("GM", 0, 128, 16))
         cp(ALL("thf"), ALL("thi"))
+        fill(ALL("oneb"), 1.0)
         mm(V("pM", 128, 133), ALL("GE"), ALL("thf"))
+        line(ALL("CQ"), (T["colc"][0:1, 0:128], [("colc", 0, 128)]), -0.25, 31.75)
+        line(V("C2", 0, 128), V("colc", 0, 128), -0.5, 130560.0 + 63.5)
+        ts(V("DM", 0, 128), V("mod16", 0, 128), V("p16", 0, 1), ALU.is_equal)
+        ts(V("ND", 0, 128), V("mod16", 0, 128), V("p16", 0, 1), ALU.not_equal)
+        fill(V("ND", 128, 144), 1.0)
+        ts(V("dump", 0, 8), V("dump0", 0, 8), V("p16", 0, 1), ALU.add)
+        ts(V("OW1", 128, 256), V("dumpw", 0, 128), V("p16", 0, 1), ALU.add)
+        ts(V("OW0", 128, 256), V("dumpw", 0, 128), V("p16", 0, 1), ALU.add)
+        fill(V("GD", 192, 208), 0.0)
         ts(V("LM", 0, 5), V("pM", 128, 133), 32.0, ALU.mult, 31.75, ALU.add)
-        fill(V("OW0", 128, 256), 0.0)
-        fill(V("OW1", 128, 256), 0.0)
 
     for s in range(S):
         par, nxp = s % 2, (s + 1) % 2
         last = s == S - 1
         zr, nr, hr, zs1 = "ZR%d" % s, "NR%d" % s, "HR%d" % s, "ZS%d" % (s + 1)
+        nold = "NS0" if s == 0 else "NR%d" % (s - 1)
         send("OU%d" % (s + 1), "OU%d" % s, 0, 128, "rO%d" % s)
         send(zr, "ZS%d" % s, 0, 192, "rZ%d" % s)
-        reduce16("PG", 0, 64, "WP", PB[0])
-        if s > 0:
-            mm(V("pM", 136, 137), V("GM", 0, 128), V("rs", 0, 1))
-            line(V("A32", 0, 1), V("pM", 136, 137), 32.0, -8388608.0 - 1184.0)
-            line(V("Q32", 0, 128), V("OW%d" % par, 0, 128), 1184.0, V("A32", 0, 1))
-        else:
-            line(V("OQ0", 0, 128), V("OW0", 0, 128), 1.0 / 32, -1.0 / 32)
-            line(V("Q32", 0, 128), V("OW0", 0, 128), 1184.0, -8388608.0 - 1184.0)
-        reduce16("PG", 64, 128, "WP", PB[1])
+        for half in (0, 1):
+            a, b = 64 * half, 64 * half + 64
+            reduce16("PG", a, b, "WP", PB[half], (V("NI", 0, 128), V(nold, a, b)))
+            if half == 0 and s > 0:
+                ts(V("MB", 64, 128), V("ZS%d" % s, 128, 192), float(s), ALU.is_gt)
+                op("v", lambda: g.vector.tensor_reduce(out=T["rs"][:, 0:1], in_=T["pS"][:, 0:128], axis=AxisListType.X, op=ALU.add),
+                   [V("pS", 0, 128)], [V("rs", 0, 1)])
+                mm(V("pM", 136, 137), V("GM", 0, 128), V("rs", 0, 1))
 
         def road(half):
             a, b = 64 * half, 64 * half + 64
             tt(V("pS", 384 + a, 384 + b), V(PB[half], 0, 64), V("MB", a, b), ALU.mult)
-            tt(V("R1", a, b), V("pS", 384 + a, 384 + b), V("NM", a, b), ALU.add)
+            tt(V("R1", a, b), V("pS", 384 + a, 384 + b), V(nold, a, b), ALU.add)
             cp(V("RU", a, b), V("R1", a, b))
 
         road(0)
         for L in (0, 1):
             for j in (0, 1):
                 gather_abs(L, j, "RU", "ztb")
-        reduce16("AB", 0, 64, "W", "pUA")
+        reduce16("AB", 0, 64, "W", "pUA", None)
+        if s > 0:
+            line(V("A32", 0, 1), V("pM", 136, 137), 32.0, A0)
+            line(V("Q32", 0, 128), V("OW%d" % par, 0, 128), 1184.0, V("A32", 0, 1))
+        else:
+            line(V("OQ0", 0, 128), V("OW0", 0, 128), 1.0 / 32, -1.0 / 32)
+            line(V("Q32", 0, 128), V("OW0", 0, 128), 1184.0, A0)
         road(1)
         for j in (0, 1):
             gather_abs(2, j, "RU", "ztb")
-        reduce16("AB", 64, 96, "W", "pUB")
+        reduce16("AB", 64, 96, "W", "pUB", None)
         gather_abs(3, 0, "RU", "ztb")
         h_of(0, s)
         gather_abs(3, 1, "RU", "ztb")
-        reduce16("AB", 96, 128, "W", "pUC")
+        reduce16("AB", 96, 128, "W", "pUC", None)
         h_of(1, s)
         if s > 0:
             tt(V("pS", 128, 256), V("pS", 0, 128), V("hN", 0, 128), ALU.mult)
             tt(V("NS%d" % s, 0, 128), V("pS", 128, 256), V("NR%d" % (s - 1), 0, 128), ALU.add)
         date = V(zr, 64, 192)
-        tile0("ztc", zr)
-        tile1("ztc")
+        tile("ztc", zr)
+        tile_end("ztc")
+        if s == 0:
+            late_constants()
 
         def known():
             cp(V("OW%d" % nxp, 0, 128), V("OU%d" % (s + 1), 0, 128))
@@ -340,10 +344,7 @@ def rank_program(g, core, T, topo):
         h_of(2, s)
         send(nr, "NS%d" % s, 0, 128, "rN%d" % s)
         if s == 0:
-            late_constants()
             known()
-        tt(V("RT0", 0, 128), V("e1", 0, 128), V("e2", 0, 128), ALU.mult)
-        ts(V("RT", 0, 128), V("RT0", 0, 128), V("LM", s, s + 1), ALU.add)
         if last:
             dma("s", "o_lo", V("LO", 0, 256), (T["PW"][0:128:16, 1:4097], [("PW", 1, 4097)]))
             dma("s", "o_hi", V("LO", 256, 512), (T["PW"][1:128:16, 1:4097], [("PW", 1, 4097)]))
@@ -355,7 +356,7 @@ def rank_program(g, core, T, topo):
                 for j in (0, 1):
                     gather_abs(L, j, hr, "ztc")
             if last and half == 0:
-                line(V("pR", 256, 512), V("LO", 256, 512), 64.0, -1.0)
+                line(V("pR", 256, 512), V("LO", 256, 512), 1.0, -1.0)
             reduce16("AB", a, b, "W", KB[half], (ALL("oneb"), (T["CQ"][:, a:b], [("CQ", a, b)])))
         cp(V("HW", 0, 128), V(hr, 0, 128))
 
@@ -366,88 +367,92 @@ def rank_program(g, core, T, topo):
             scan(V("SM", a, b), V("SEG32", a, b), kd, ALU.mult, ALU.max)
             scan(V("SM", 128 + a, 128 + b), V("SEG32", a, b), V("K2", a, b), ALU.mult, ALU.max)
 
-        def redeem(half):
+        def redeem(half, n):
             a, b = 64 * half, 64 * half + 64
-            tt(V("pS", a, b), V(KB[half], 0, 64), V("RT", a, b), ALU.is_le)
-            tt(V("pS", 128 + a, 128 + b), V("pS", a, b), V("ST", a, b), ALU.mult)
-            tt(V("pS", 256 + a, 256 + b), V("pS", 128 + a, 128 + b), V(zr, 64 + a, 64 + b), ALU.add)
+            if n == 0:
+                tt(V("pS", a, b), V(KB[half], 0, 64), V("RT", a, b), ALU.is_le)
+            elif n == 1:
+                tt(V("pS", 128 + a, 128 + b), V("pS", a, b), V("ST", a, b), ALU.mult)
+            else:
+                tt(V("pS", 256 + a, 256 + b), V("pS", 128 + a, 128 + b), V(zr, 64 + a, 64 + b), ALU.add)
+
+        def refuse(L):
+            ts(V("RF", 32 * L, 32 * L + 32), V(KB[L // 2], 32 * (L % 2), 32 * (L % 2) + 32), V("gk", L, L + 1),
+               ALU.is_equal, 99.0, ALU.mult)
+
+        def newdate(half):
+            a, b = 64 * half, 64 * half + 64
+            tt(V(zs1, 64 + a, 64 + b), V("pS", 256 + a, 256 + b), V("RF", a, b), ALU.max)
 
         if last:
             tt(V("YPg", 0, 256), V("pR", 256, 512), V("LO", 0, 256), ALU.add)
             dma("s", "o_pf", (T["PF"][0:128:16, 1:4097], [("PF", 1, 4097)]), V("YPg", 0, 256))
+        tt(V("RT0", 0, 128), V("e1", 0, 128), V("e2", 0, 128), ALU.mult)
         keys(0)
-        redeem(0)
+        ts(V("RT", 0, 128), V("RT0", 0, 128), V("LM", s, s + 1), ALU.add)
         tt(V("hN", 0, 128), V("HW", 0, 128), V(nr, 0, 128), ALU.subtract)
+        redeem(0, 0)
+        redeem(0, 1)
+        redeem(0, 2)
         keys(1)
         lastk = V("SM", 31, 128, 32)
-        ts(V("KI", 0, 8), V("SM", 31, 256, 32), 4.0, ALU.mult)
         ts(V("nogo", 0, 4), lastk, V("LM", s, s + 1), ALU.is_le, 128.0, ALU.mult)
+        ts(V("KI", 0, 8), V("SM", 31, 256, 32), 4.0, ALU.mult)
+        redeem(1, 0)
         ts(V("CI", 0, 8), V("KI", 0, 8), 127, ALU.bitwise_and)
+        tt(V("gk", 0, 4), lastk, V("nogo", 0, 4), ALU.subtract)
         tt(V("CI", 8, 12), V("CI", 0, 4), V("nogo", 0, 4), ALU.subtract)
+        redeem(1, 1)
         ts(V("OFF", 0, 12), V("CI", 0, 12), -1.0, ALU.mult, 127.0, ALU.add)
+        redeem(1, 2)
         tt(V("GD", 0, 128), IND(V("HW", 0, 128), V("OFF", 0, 8)), V("DM", 0, 128), ALU.mult)
         tt(V("GD", 128, 192), IND(V("OW%d" % nxp, 0, 256), V("OFF", 8, 12)), V("DM", 0, 64), ALU.mult)
-        mm(V("pR", 0, 64), V("LT", 0, 128), V("GD", 128, 192))
+        mm(V("pM", 0, 128), V("LT", 0, 128), V("GD", 64, 192))
         mm(V("pR", 64, 128), V("GM", 0, 128), V("GD", 0, 64))
-        if not last:
-            mm(V("pR", 128, 192), V("GL", 0, 128), V("GD", 0, 64))
-        mm(V("pM", 0, 64), V("LT", 0, 128), V("GD", 64, 128))
-        scan(V("OWN", 64, 192), V("SEG16", 0, 128), V("GD", 64, 192), ALU.mult, ALU.add)
-        cp(V("HB", 0, 4), V("OWN", 79, 128, 16))
+        refuse(0)
+        scan(V("OWN", 0, 144), V("ND", 0, 144), V("GD", 64, 208), ALU.mult, ALU.add)
+        refuse(1)
+        cp(V("HB", 0, 4), V("OWN", 15, 64, 16))
+        refuse(2)
         tt(V("gz", 0, 64), IND(XR, V("HB", 0, 4)), V(zr, 0, 64), ALU.add)
+        refuse(3)
         ts(V("zi", 0, 64), V("gz", 0, 64), 0.5, ALU.mult, -0.25, ALU.add)
         cp(V(zs1, 0, 64), V("zi", 0, 64))
-
-        def resolve(e, f, fin, fu, bank, own):
-            for L in range(4):
-                ts(V(e, 16 * L, 16 * L + 16), V(bank, 16 * L, 16 * L + 16), V("OWN", own + 16 * L + 15, own + 16 * L + 16),
-                   ALU.is_equal, V("dump", L, L + 1), ALU.mult)
-            scan(V(f, 0, 64), V("SEG16", 0, 64), V(e, 0, 64), ALU.mult, ALU.max)
-            tt(V(fin, 0, 4), V(f, 15, 64, 16), V("OWN", own + 15, own + 64, 16), ALU.max)
-            cp(V(fu, 0, 8, 2), V(fin, 0, 4))
+        if not last:
+            tile("ztb", zs1)
+        else:
+            dma("a", "o_z", ALL("yz"), V(zs1, 0, 64))
+        tt(V("E", 0, 128), V("OWN", 16, 144), V("pM", 0, 128), ALU.is_equal)
+        if not last:
+            ts(V("hx", 0, 64), V("pR", 64, 128), V("q1", 0, 1), ALU.mult)
+        scan(V("F", 0, 128), V("SEG16", 0, 128), V("E", 0, 128), ALU.mult, ALU.max)
+        if not last:
+            tt(V("PD", 0, 64), V("pR", 64, 128), V("hx", 0, 64), ALU.subtract)
+        else:
+            ts(V("ht", 0, 64), V("pR", 64, 128), -1.0, ALU.add)
+        tt(V("f1", 0, 8), V("F", 15, 128, 16), V("dump", 0, 8), ALU.mult)
+        newdate(0)
+        tt(V("f2", 0, 8), V("f1", 0, 8), V("OWN", 15, 128, 16), ALU.max)
+        newdate(1)
+        cp(V("fu", 0, 16, 2), V("f2", 0, 8))
 
         def write(win, fu, data):
             for L in (3, 2, 1, 0):
-                cp(IND(win, V(fu, 2 * L, 2 * L + 1)), V(data, 16 * L, 16 * L + 16))
-
-        def items():
-            resolve("EX", "FX", "fx", "fxu", "pM", 64)
-            write(XA, "fxu", "zi")
-
-        def dates():
-            redeem(1)
-            tt(V("gk", 0, 4), lastk, V("nogo", 0, 4), ALU.subtract)
-            for L in range(4):
-                ts(V("RF", 32 * L, 32 * L + 32), V(KB[L // 2], 32 * (L % 2), 32 * (L % 2) + 32), V("gk", L, L + 1),
-                   ALU.is_equal, 99.0, ALU.mult)
-            tt(V(zs1, 64, 192), V("pS", 256, 384), V("RF", 0, 128), ALU.max)
+                cp(IND(win, V("fu", fu + 2 * L, fu + 2 * L + 1)), V(data, 16 * L, 16 * L + 16))
 
         if not last:
-            tile0("ztb", zs1)
-            ts(V("hi", 0, 64), V("pR", 64, 128), -31.5, ALU.add, 1.0 / 64, ALU.mult)
-            resolve("EP", "FP", "fp", "fpu", "pR", 128)
-            ts(V("ht", 0, 64), V("hi", 0, 64), V("beta", 0, 1), ALU.mult)
-            tt(V("PD", 0, 64), V("pR", 128, 192), V("ht", 0, 64), ALU.add)
-            write(PA, "fpu", "PD")
-            act(*pgather(s + 1, 0))
-            tile1("ztb")
-            act(*pgather(s + 1, 1))
-            dates()
-            op("v", lambda: g.vector.tensor_reduce(out=T["rs"][:, 0:1], in_=T["pS"][:, 0:128], axis=AxisListType.X, op=ALU.add),
-               [V("pS", 0, 128)], [V("rs", 0, 1)])
-            ts(V("MB", 0, 128), V(zs1, 64, 192), float(s + 1), ALU.is_gt)
-            ts(V("pS", 384, 512), V(zs1, 64, 192), float(s + 1), ALU.is_le)
-            tt(V("NM", 0, 128), V("pS", 384, 512), V(nr, 0, 128), ALU.mult)
-            items()
+            ts(V("MB", 0, 64), V(zs1, 64, 128), float(s + 1), ALU.is_gt)
+            write(PA, 8, "PD")
+            act(*pgather(s + 1, 0, 32))
+            cp(*pgather(s + 1, 32, 64))
+            tile_end("ztb")
+            act(*pgather(s + 1, 64, 128))
+            write(XA, 0, "zi")
         else:
-            dma("a", "o_z", ALL("yz"), V(zs1, 0, 64))
-            items()
+            write(XA, 0, "zi")
             dma("s", "o_x", ALL("yx"), V("XW", 1, 4097))
-            resolve("EP", "FP", "fp", "fpu", "pR", 128)
-            ts(V("ht", 0, 64), V("pR", 64, 128), -1.0, ALU.add)
-            write(V("PF", 0, PADW), "fpu", "ht")
+            write(V("PF", 0, PADW), 8, "ht")
             dma("a", "o_p", ALL("yp"), (T["PF"][0:128:16, 1:4097], [("PF", 1, 4097)]))
-            dates()
             for L in range(4):
                 cp(V("YT", L, 128, 4), V(zs1, 64 + 32 * L, 96 + 32 * L))
             dma("a", "o_t", ALL("yt"), V("YT", 0, 128))

@@ -16,13 +16,13 @@ SCRATCH = {
     "pxi": _sb(256, "int32"), "pxt": _sb(256, "int32"), "LH": _sb(512, "bfloat16"),
     "oli": _sb(128, "int32"), "nli": _sb(128, "int32"), "tli": _sb(128, "int32"),
     "thi": _sb(5, "int32", 8), "thf": _sb(5, "float32", 8), "GE1": _sb(128, "float32", 8), "GE": _sb(128, "float32", 8),
-    "ones": _sb(128), "neg": _sb(128), "oneb": _sb(128, "bfloat16", 1), "CQ": _sb(128, "bfloat16", 1),
-    "one2": _sb(192), "G1": _sb(128), "GM": _sb(128), "NI": _sb(128), "LT": _sb(128), "GA": _sb(8), "GP": _sb(8),
+    "ones": _sb(128), "oneb": _sb(128, "bfloat16", 1), "CQ": _sb(128, "bfloat16", 1),
+    "G1": _sb(128), "GM": _sb(128), "ID": _sb(128), "LT": _sb(128), "GA": _sb(8), "GP": _sb(8),
     "mod16": _sb(128), "colc": _sb(128), "C2": _sb(128), "SEG16": _sb(128), "SEG32": _sb(128), "DM": _sb(128), "ND": _sb(144),
     "pidx": _sb(1, "int32"), "p16i": _sb(1, "int32"), "p16": _sb(1), "q0": _sb(1), "q1": _sb(1), "wp": _sb(1),
     "dump0": _sb(8), "dump": _sb(8), "dumpw": _sb(128), "LM": _sb(5),
     "OW0": _sb(256), "OW1": _sb(256), "OQ0": _sb(128), "OQ1": _sb(128), "HW": _sb(128), "Q32": _sb(128), "A32": _sb(1), "rs": _sb(1),
-    "MB": _sb(128), "R1": _sb(128), "RU": _sb(128, "uint16"),
+    "om": _sb(128), "OM": _sb(128, "uint16"), "NM": _sb(128), "RU": _sb(128, "uint16"),
     "hm": _sb(128), "hv": _sb(128, "int32"), "hs": _sb(128, "int32"),
     "e1": _sb(128), "e2": _sb(128), "RT0": _sb(128), "RT": _sb(128), "ST": _sb(128), "hN": _sb(128), "K2": _sb(128), "SM": _sb(256),
     "KI": _sb(8, "int32"), "CI": _sb(12, "int32"), "nogo": _sb(4, "int32"), "gk": _sb(4), "OFF": _sb(12, "uint16"),
@@ -173,18 +173,20 @@ def rank_program(g, core, T, topo):
     XR, PR = V("XW", 0, 4112), V("PW", 0, 4112)
     XA, PA = V("XW", 0, PADW), V("PW", 0, PADW)
 
-    def tile(name, src):
+    def tile(name, src, steps=(0, 16, 32, 64)):
         t = T[name]
-        act((t[:, :, 0:16], [(name, 0, 16)]), V(src, 0, 64))
-        for w in (16, 32, 64):
-            act((t[:, :, w:2 * w], [(name, w, 2 * w)]), (t[:, :, 0:w], [(name, 0, w)]))
+        for w in steps:
+            if w == 0:
+                act((t[:, :, 0:16], [(name, 0, 16)]), V(src, 0, 64))
+            else:
+                act((t[:, :, w:2 * w], [(name, w, 2 * w)]), (t[:, :, 0:w], [(name, 0, w)]))
 
-    def tile_end(name):
+    def tile_end(name, copy):
         t = T[name]
-        act((t[:, :, 128:256], [(name, 128, 256)]), (t[:, :, 0:128], [(name, 0, 128)]))
+        copy((t[:, :, 128:256], [(name, 128, 256)]), (t[:, :, 0:128], [(name, 0, 128)]))
 
-    def pgather(s, a, b):
-        return V("PG", 16 * a, 16 * b), IND(PR, V("OU%d" % s, a, b))
+    def pgather(a, b):
+        return V("PG", 16 * a, 16 * b), IND(PR, V("OM", a, b))
 
     def reduce16(src, c0, c1, w, bank, first):
         out = V(bank, 0, c1 - c0)
@@ -199,11 +201,13 @@ def rank_program(g, core, T, topo):
         tt(V("DF", lo, lo + TW), IND(XR, V(off, lo // 16, (lo + TW) // 16)), (T[tname][:, L, 0:TW], [(tname, 0, TW)]), ALU.subtract)
         act(V("AB", lo, lo + TW), V("DF", lo, lo + TW), ACT.Abs)
 
-    def h_of(piece, s):
+    def h_of(piece, s, between=None):
         a, b, bank, sem = HP[piece]
         u = V(bank, 0, b - a)
         tt(V("hm", a, b), u, V("OQ%d" % (s % 2), a, b), ALU.mult)
         tt(V("pS", 256 + a, 256 + b), u, V("Q32", a, b), ALU.add)
+        if between is not None:
+            between()
         tt(V("hv", a, b), V("pS", 256 + a, 256 + b), V("hm", a, b), ALU.add)
         ts(V("hs", a, b), V("hv", a, b), 5, ALU.arith_shift_right, 4095, ALU.bitwise_and)
         ts(V("HS%d" % s, a, b), V("hs", a, b), 1.0, ALU.add)
@@ -212,50 +216,53 @@ def rank_program(g, core, T, topo):
     dma("s", "d_px", V("pxi", 0, 256), ALL("px"))
     dma("a", "d_ol", V("oli", 0, 128), ALL("ol"))
     dma("s", "d_z", V("ZS0", 0, 64), ALL("z"))
-    dma("a", "d_nl", V("nli", 0, 128), ALL("nl"))
+    dma("a", "d_tl", V("tli", 0, 128), ALL("tl"))
     fill(V("ones", 0, 128), 1.0)
     fill(V("XW", 0, 16), 0.0)
     fill(V("XW", 4096, PADW), 0.0)
     dma("s", "d_x", V("XW", 1, 4097), ALL("x"))
-    dma("a", "d_tl", V("tli", 0, 128), ALL("tl"))
+    dma("a", "d_nl", V("nli", 0, 128), ALL("nl"))
     dma("a", "d_th", ALL("thi"), ALL("th"))
-    fill(V("neg", 0, 128), -1.0)
     iota(V("pidx", 0, 1), [[0, 1]], 0, 1)
     select(V("G1", 0, 128), V("ones", 0, 128), [[-16, 8], [0, 16]], ALU.is_ge, 0, 1)
     select(V("GM", 0, 128), V("G1", 0, 128), [[16, 8], [0, 16]], ALU.is_ge, 15, -1)
-    select(V("NI", 0, 128), V("neg", 0, 128), [[1, 128]], ALU.is_equal, 0, -1)
+    select(V("ID", 0, 128), V("ones", 0, 128), [[1, 128]], ALU.is_equal, 0, -1)
     iota(V("W", 0, 2048), [[0, 2048]], 0, 0)
     fill(V("PW", 0, PADW), 0.0)
     ts(V("LH", 256, 512), V("pxi", 0, 256), 1, ALU.add)
     waits("a", [("LH", 256, 512), ("PW", 0, PADW)], [])
     g.scalar.dma_start(out=T["PW"][1:128:16, 1:4097], in_=T["LH"][:, 256:512]).then_inc(T.sem["d_hi"], 16)
     ts(V("pxt", 0, 256), V("pxi", 0, 256), 1, ALU.add)
+    ts(V("p16i", 0, 1), V("pidx", 0, 1), 15, ALU.bitwise_and)
     tt(V("LH", 0, 256), V("pxt", 0, 256), V("LH", 256, 512), ALU.subtract)
     dma("s", "d_lo", (T["PW"][0:128:16, 1:4097], [("PW", 1, 4097)]), V("LH", 0, 256))
     note("dd_hi", "d_hi", 16, [("LH", 256, 512)], False)
     acc["PW"] = acc["PW"] + [("dd_hi", "d_hi", 16, 1, 4097, True)]
-    for L in range(4):
-        ts(V("OW0", 32 * L, 32 * L + 32), V("oli", L, 128, 4), 1, ALU.add)
-    cp(V("OU0", 0, 128), V("OW0", 0, 128))
-    fill(V("WP", 0, 2048), 0.0)
-    ts(V("p16i", 0, 1), V("pidx", 0, 1), 15, ALU.bitwise_and)
-    for L in range(4):
-        ts(V("NS0", 32 * L, 32 * L + 32), V("nli", L, 128, 4), 1, ALU.add)
     cp(V("p16", 0, 1), V("p16i", 0, 1))
-    ts(V("GA", 0, 8), V("GM", 0, 128, 16), 32.0, ALU.mult)
-    ts(V("q0", 0, 1), V("p16", 0, 1), 0.0, ALU.is_equal)
-    ts(V("q1", 0, 1), V("p16", 0, 1), 1.0, ALU.is_equal)
-    tt(V("wp", 0, 1), V("q1", 0, 1), V("q0", 0, 1), ALU.add)
-    ts(V("GP", 0, 8), V("GM", 0, 128, 16), V("wp", 0, 1), ALU.mult)
-    for i in range(16):
-        cp(V("WP", 128 * i + i, 128 * i + 128, 16), V("GP", 0, 8))
-    tile("ztb", "ZS0")
-    tile_end("ztb")
-    act(*pgather(0, 0, 64))
     for L in range(4):
         cp(V("ZS0", 64 + 32 * L, 96 + 32 * L), V("tli", L, 128, 4))
-    cp(*pgather(0, 64, 128))
-    ts(V("MB", 0, 128), V("ZS0", 64, 192), 0.0, ALU.is_gt)
+    ts(V("q0", 0, 1), V("p16", 0, 1), 0.0, ALU.is_equal)
+    ts(V("q1", 0, 1), V("p16", 0, 1), 1.0, ALU.is_equal)
+    for L in range(4):
+        ts(V("OW0", 32 * L, 32 * L + 32), V("oli", L, 128, 4), 1, ALU.add)
+    ts(V("pS", 384, 512), V("ZS0", 64, 192), 0.0, ALU.is_gt)
+    tt(V("wp", 0, 1), V("q1", 0, 1), V("q0", 0, 1), ALU.add)
+    ts(V("GA", 0, 8), V("GM", 0, 128, 16), 32.0, ALU.mult)
+    tt(V("om", 0, 128), V("pS", 384, 512), V("OW0", 0, 128), ALU.mult)
+    ts(V("GP", 0, 8), V("GM", 0, 128, 16), V("wp", 0, 1), ALU.mult)
+    fill(V("WP", 0, 2048), 0.0)
+    cp(V("OM", 0, 128), V("om", 0, 128))
+    ts(V("pS", 256, 384), V("ZS0", 64, 192), 0.0, ALU.is_le)
+    for i in range(16):
+        cp(V("WP", 128 * i + i, 128 * i + 128, 16), V("GP", 0, 8))
+    for L in range(4):
+        ts(V("NS0", 32 * L, 32 * L + 32), V("nli", L, 128, 4), 1, ALU.add)
+    cp(V("OU0", 0, 128), V("OW0", 0, 128))
+    tt(V("NM", 0, 128), V("pS", 256, 384), V("NS0", 0, 128), ALU.mult)
+    tile("ztb", "ZS0")
+    tile_end("ztb", act)
+    act(*pgather(0, 64))
+    cp(*pgather(64, 128))
     for i in range(16):
         act(V("W", 128 * i + i, 128 * i + 128, 16), V("GA", 0, 8))
     select(V("LT", 0, 128), V("GM", 0, 128), [[1, 128]], ALU.is_gt, 0, -1)
@@ -287,25 +294,14 @@ def rank_program(g, core, T, topo):
         par, nxp = s % 2, (s + 1) % 2
         last = s == S - 1
         zr, nr, hr, zs1 = "ZR%d" % s, "NR%d" % s, "HR%d" % s, "ZS%d" % (s + 1)
-        nold = "NS0" if s == 0 else "NR%d" % (s - 1)
         send("OU%d" % (s + 1), "OU%d" % s, 0, 128, "rO%d" % s)
         send(zr, "ZS%d" % s, 0, 192, "rZ%d" % s)
         for half in (0, 1):
             a, b = 64 * half, 64 * half + 64
-            reduce16("PG", a, b, "WP", PB[half], (V("NI", 0, 128), V(nold, a, b)))
+            reduce16("PG", a, b, "WP", PB[half], (V("ID", 0, 128), V("NM", a, b)))
             if half == 0 and s > 0:
-                ts(V("MB", 64, 128), V("ZS%d" % s, 128, 192), float(s), ALU.is_gt)
-                op("v", lambda: g.vector.tensor_reduce(out=T["rs"][:, 0:1], in_=T["pS"][:, 0:128], axis=AxisListType.X, op=ALU.add),
-                   [V("pS", 0, 128)], [V("rs", 0, 1)])
                 mm(V("pM", 136, 137), V("GM", 0, 128), V("rs", 0, 1))
-
-        def road(half):
-            a, b = 64 * half, 64 * half + 64
-            tt(V("pS", 384 + a, 384 + b), V(PB[half], 0, 64), V("MB", a, b), ALU.mult)
-            tt(V("R1", a, b), V("pS", 384 + a, 384 + b), V(nold, a, b), ALU.add)
-            cp(V("RU", a, b), V("R1", a, b))
-
-        road(0)
+        cp(V("RU", 0, 64), V(PB[0], 0, 64))
         for L in (0, 1):
             for j in (0, 1):
                 gather_abs(L, j, "RU", "ztb")
@@ -313,24 +309,27 @@ def rank_program(g, core, T, topo):
         if s > 0:
             line(V("A32", 0, 1), V("pM", 136, 137), 32.0, A0)
             line(V("Q32", 0, 128), V("OW%d" % par, 0, 128), 1184.0, V("A32", 0, 1))
+            tt(V("pS", 128, 256), V("pS", 0, 128), V("hN", 0, 128), ALU.mult)
+            cp(V("RU", 64, 128), V(PB[1], 0, 64))
+            tt(V("NS%d" % s, 0, 128), V("pS", 128, 256), V("NR%d" % (s - 1), 0, 128), ALU.add)
         else:
             line(V("OQ0", 0, 128), V("OW0", 0, 128), 1.0 / 32, -1.0 / 32)
             line(V("Q32", 0, 128), V("OW0", 0, 128), 1184.0, A0)
-        road(1)
+            cp(V("RU", 64, 128), V(PB[1], 0, 64))
         for j in (0, 1):
             gather_abs(2, j, "RU", "ztb")
+            if s > 0:
+                tile("ztc", zr, ((0,), (16,))[j])
         reduce16("AB", 64, 96, "W", "pUB", None)
         gather_abs(3, 0, "RU", "ztb")
-        h_of(0, s)
-        gather_abs(3, 1, "RU", "ztb")
-        reduce16("AB", 96, 128, "W", "pUC", None)
-        h_of(1, s)
         if s > 0:
-            tt(V("pS", 128, 256), V("pS", 0, 128), V("hN", 0, 128), ALU.mult)
-            tt(V("NS%d" % s, 0, 128), V("pS", 128, 256), V("NR%d" % (s - 1), 0, 128), ALU.add)
+            tile("ztc", zr, (32,))
+        h_of(0, s, lambda: gather_abs(3, 1, "RU", "ztb"))
+        reduce16("AB", 96, 128, "W", "pUC", None)
+        tile("ztc", zr, (64,) if s > 0 else (0, 16, 32, 64))
+        tile_end("ztc", act)
+        h_of(1, s)
         date = V(zr, 64, 192)
-        tile("ztc", zr)
-        tile_end("ztc")
         if s == 0:
             late_constants()
 
@@ -360,11 +359,13 @@ def rank_program(g, core, T, topo):
             reduce16("AB", a, b, "W", KB[half], (ALL("oneb"), (T["CQ"][:, a:b], [("CQ", a, b)])))
         cp(V("HW", 0, 128), V(hr, 0, 128))
 
-        def keys(half):
+        def keys(half, between=None):
             a, b = 64 * half, 64 * half + 64
             kd = V(KB[half], 0, 64)
             tt(V("K2", a, b), V("C2", a, b), kd, ALU.subtract)
             scan(V("SM", a, b), V("SEG32", a, b), kd, ALU.mult, ALU.max)
+            if between is not None:
+                between()
             scan(V("SM", 128 + a, 128 + b), V("SEG32", a, b), V("K2", a, b), ALU.mult, ALU.max)
 
         def redeem(half, n):
@@ -384,6 +385,23 @@ def rank_program(g, core, T, topo):
             a, b = 64 * half, 64 * half + 64
             tt(V(zs1, 64 + a, 64 + b), V("pS", 256 + a, 256 + b), V("RF", a, b), ALU.max)
 
+        def onward(n):
+            if last:
+                return
+            if n == 0:
+                ts(V("pS", 384, 512), V(zs1, 64, 192), float(s + 1), ALU.is_gt)
+            elif n == 1:
+                ts(V("pS", 256, 384), V(zs1, 64, 192), float(s + 1), ALU.is_le)
+            elif n == 2:
+                tt(V("om", 0, 128), V("pS", 384, 512), V("OW%d" % nxp, 0, 128), ALU.mult)
+            elif n == 3:
+                cp(V("OM", 0, 128), V("om", 0, 128))
+            else:
+                tt(V("NM", 0, 128), V("pS", 256, 384), V(nr, 0, 128), ALU.mult)
+
+        def write(L, win, fu, data):
+            cp(IND(win, V("fu", fu + 2 * L, fu + 2 * L + 1)), V(data, 16 * L, 16 * L + 16))
+
         if last:
             tt(V("YPg", 0, 256), V("pR", 256, 512), V("LO", 0, 256), ALU.add)
             dma("s", "o_pf", (T["PF"][0:128:16, 1:4097], [("PF", 1, 4097)]), V("YPg", 0, 256))
@@ -391,76 +409,78 @@ def rank_program(g, core, T, topo):
         keys(0)
         ts(V("RT", 0, 128), V("RT0", 0, 128), V("LM", s, s + 1), ALU.add)
         tt(V("hN", 0, 128), V("HW", 0, 128), V(nr, 0, 128), ALU.subtract)
-        redeem(0, 0)
-        redeem(0, 1)
-        redeem(0, 2)
-        keys(1)
+        for n in (0, 1, 2):
+            redeem(0, n)
+        keys(1, lambda: redeem(1, 0))
         lastk = V("SM", 31, 128, 32)
         ts(V("nogo", 0, 4), lastk, V("LM", s, s + 1), ALU.is_le, 128.0, ALU.mult)
+        redeem(1, 1)
         ts(V("KI", 0, 8), V("SM", 31, 256, 32), 4.0, ALU.mult)
-        redeem(1, 0)
         ts(V("CI", 0, 8), V("KI", 0, 8), 127, ALU.bitwise_and)
         tt(V("gk", 0, 4), lastk, V("nogo", 0, 4), ALU.subtract)
+        ts(V("OFF", 0, 8), V("CI", 0, 8), -1.0, ALU.mult, 127.0, ALU.add)
         tt(V("CI", 8, 12), V("CI", 0, 4), V("nogo", 0, 4), ALU.subtract)
-        redeem(1, 1)
-        ts(V("OFF", 0, 12), V("CI", 0, 12), -1.0, ALU.mult, 127.0, ALU.add)
         redeem(1, 2)
         tt(V("GD", 0, 128), IND(V("HW", 0, 128), V("OFF", 0, 8)), V("DM", 0, 128), ALU.mult)
+        ts(V("OFF", 8, 12), V("CI", 8, 12), -1.0, ALU.mult, 127.0, ALU.add)
+        refuse(0)
         tt(V("GD", 128, 192), IND(V("OW%d" % nxp, 0, 256), V("OFF", 8, 12)), V("DM", 0, 64), ALU.mult)
         mm(V("pM", 0, 128), V("LT", 0, 128), V("GD", 64, 192))
         mm(V("pR", 64, 128), V("GM", 0, 128), V("GD", 0, 64))
-        refuse(0)
         scan(V("OWN", 0, 144), V("ND", 0, 144), V("GD", 64, 208), ALU.mult, ALU.add)
         refuse(1)
         cp(V("HB", 0, 4), V("OWN", 15, 64, 16))
         refuse(2)
-        tt(V("gz", 0, 64), IND(XR, V("HB", 0, 4)), V(zr, 0, 64), ALU.add)
         refuse(3)
-        ts(V("zi", 0, 64), V("gz", 0, 64), 0.5, ALU.mult, -0.25, ALU.add)
-        cp(V(zs1, 0, 64), V("zi", 0, 64))
-        if not last:
-            tile("ztb", zs1)
-        else:
-            dma("a", "o_z", ALL("yz"), V(zs1, 0, 64))
+        tt(V("gz", 0, 64), IND(XR, V("HB", 0, 4)), V(zr, 0, 64), ALU.add)
         tt(V("E", 0, 128), V("OWN", 16, 144), V("pM", 0, 128), ALU.is_equal)
+        ts(V("zi", 0, 64), V("gz", 0, 64), 0.5, ALU.mult, -0.25, ALU.add)
         if not last:
             ts(V("hx", 0, 64), V("pR", 64, 128), V("q1", 0, 1), ALU.mult)
         scan(V("F", 0, 128), V("SEG16", 0, 128), V("E", 0, 128), ALU.mult, ALU.max)
+        cp(V(zs1, 0, 64), V("zi", 0, 64))
         if not last:
+            tile("ztb", zs1)
             tt(V("PD", 0, 64), V("pR", 64, 128), V("hx", 0, 64), ALU.subtract)
         else:
+            dma("a", "o_z", ALL("yz"), V(zs1, 0, 64))
             ts(V("ht", 0, 64), V("pR", 64, 128), -1.0, ALU.add)
         tt(V("f1", 0, 8), V("F", 15, 128, 16), V("dump", 0, 8), ALU.mult)
         newdate(0)
-        tt(V("f2", 0, 8), V("f1", 0, 8), V("OWN", 15, 128, 16), ALU.max)
         newdate(1)
+        tt(V("f2", 0, 8), V("f1", 0, 8), V("OWN", 15, 128, 16), ALU.max)
+        onward(0)
         cp(V("fu", 0, 16, 2), V("f2", 0, 8))
-
-        def write(win, fu, data):
-            for L in (3, 2, 1, 0):
-                cp(IND(win, V("fu", fu + 2 * L, fu + 2 * L + 1)), V(data, 16 * L, 16 * L + 16))
-
+        onward(1)
         if not last:
-            ts(V("MB", 0, 64), V(zs1, 64, 128), float(s + 1), ALU.is_gt)
-            write(PA, 8, "PD")
-            act(*pgather(s + 1, 0, 32))
-            cp(*pgather(s + 1, 32, 64))
-            tile_end("ztb")
-            act(*pgather(s + 1, 64, 128))
-            write(XA, 0, "zi")
+            for L in (3, 2, 1, 0):
+                write(L, PA, 8, "PD")
+                if L:
+                    onward(5 - L)
+            act(*pgather(0, 32))
+            cp(*pgather(32, 64))
+            act(*pgather(64, 112))
+            write(3, XA, 0, "zi")
+            tile_end("ztb", cp)
+            write(2, XA, 0, "zi")
+            op("v", lambda: g.vector.tensor_reduce(out=T["rs"][:, 0:1], in_=T["pS"][:, 0:128], axis=AxisListType.X, op=ALU.add),
+               [V("pS", 0, 128)], [V("rs", 0, 1)])
+            write(1, XA, 0, "zi")
+            cp(*pgather(112, 128))
+            write(0, XA, 0, "zi")
         else:
-            write(XA, 0, "zi")
-            dma("s", "o_x", ALL("yx"), V("XW", 1, 4097))
-            write(V("PF", 0, PADW), 8, "ht")
-            dma("a", "o_p", ALL("yp"), (T["PF"][0:128:16, 1:4097], [("PF", 1, 4097)]))
-            for L in range(4):
-                cp(V("YT", L, 128, 4), V(zs1, 64 + 32 * L, 96 + 32 * L))
-            dma("a", "o_t", ALL("yt"), V("YT", 0, 128))
             tt(V("pS", 128, 256), V("pS", 0, 128), V("hN", 0, 128), ALU.mult)
+            for L in (3, 2, 1, 0):
+                write(L, XA, 0, "zi")
+                cp(V("YT", L, 128, 4), V(zs1, 64 + 32 * L, 96 + 32 * L))
+            dma("s", "o_x", ALL("yx"), V("XW", 1, 4097))
+            dma("a", "o_t", ALL("yt"), V("YT", 0, 128))
             tt(V("NS%d" % (s + 1), 0, 128), V("pS", 128, 256), V(nr, 0, 128), ALU.add)
-            for L in range(4):
+            for L in (3, 2, 1, 0):
+                write(L, V("PF", 0, PADW), 8, "ht")
                 ts(V("YN", L, 128, 4), V("NS%d" % (s + 1), 32 * L, 32 * L + 32), -1.0, ALU.add)
-            dma("a", "o_n", ALL("yn"), V("YN", 0, 128))
+            dma("a", "o_p", ALL("yp"), (T["PF"][0:128:16, 1:4097], [("PF", 1, 4097)]))
+            dma("s", "o_n", ALL("yn"), V("YN", 0, 128))
     for q in ("v", "a", "t", "p"):
         g.wait_ge(T.sem[q], count[q])
     g.wait_ge(T.sem["loc"], sent[0])

from concourse.mybir import AluOpType as ALU, AxisListType, ActivationFunctionType as ACT

S, PADW, DUMP0, TW = 5, 4176, 4097, 256
BIG = 1.0e6


def _sb(n, dtype="float32", p=128):
    return ("sbuf", [p, n], dtype)


SCRATCH = {
    "XW": _sb(PADW, "bfloat16"), "PW": _sb(PADW, "bfloat16"), "PF": _sb(PADW),
    "ztb": ("sbuf", [128, 4, TW], "bfloat16"), "ztc": ("sbuf", [128, 4, TW], "bfloat16"),
    "DF": _sb(2048, "bfloat16"), "AB": _sb(2048, "bfloat16"), "PG": _sb(2048, "bfloat16"),
    "W": _sb(2048, "bfloat16"), "WP": _sb(2048, "bfloat16"),
    "pxi": _sb(256, "int32"), "pxt": _sb(256, "int32"), "LH": _sb(512, "bfloat16"),
    "oli": _sb(128, "int32"), "nli": _sb(128, "int32"), "tli": _sb(128, "int32"),
    "thi": _sb(5, "int32", 8), "thf": _sb(5, "float32", 8), "GE1": _sb(128, "float32", 8), "GE": _sb(128, "float32", 8),
    "ones": _sb(128), "oneb": _sb(128, "bfloat16", 1), "CQ": _sb(128, "bfloat16", 1),
    "G1": _sb(128), "GM": _sb(128), "ID": _sb(128), "LT": _sb(128), "GA": _sb(8), "GP": _sb(8),
    "mod16": _sb(128), "colc": _sb(128), "C2": _sb(128), "SEG16": _sb(128), "SEG32": _sb(128), "DM": _sb(128), "ND": _sb(144),
    "pidx": _sb(1, "int32"), "p16i": _sb(1, "int32"), "p16": _sb(1), "q0": _sb(1), "q1": _sb(1), "wp": _sb(1),
    "dump0": _sb(8), "dump": _sb(8), "dumpw": _sb(128), "LM": _sb(5),
    "OW0": _sb(256), "OW1": _sb(256), "OQ0": _sb(128), "OQ1": _sb(128), "HW": _sb(128), "Q32": _sb(128), "A32": _sb(1), "rs": _sb(1),
    "om": _sb(128), "OM": _sb(128, "uint16"), "NM": _sb(128), "RU": _sb(128, "uint16"),
    "hm": _sb(128), "hv": _sb(128, "int32"), "hs": _sb(128, "int32"),
    "e1": _sb(128), "e2": _sb(128), "RT0": _sb(128), "RT": _sb(128), "ST": _sb(128), "hN": _sb(128), "K2": _sb(128), "SM": _sb(256),
    "KI": _sb(8, "int32"), "CI": _sb(12, "int32"), "nogo": _sb(4, "int32"), "gk": _sb(4), "OFF": _sb(12, "uint16"),
    "GD": _sb(208), "OWN": _sb(144), "HB": _sb(4, "uint16"), "gz": _sb(64), "zi": _sb(64, "int32"),
    "E": _sb(128), "F": _sb(128), "f1": _sb(8), "f2": _sb(8), "fu": _sb(16, "uint16"),
    "hx": _sb(64, "bfloat16"), "ht": _sb(64), "PD": _sb(64, "bfloat16"), "RF": _sb(128),
    "YN": _sb(128), "YT": _sb(128), "YPg": _sb(256), "LO": _sb(512, "bfloat16"),
    "ZR": _sb(192 * S, "bfloat16"),
    "NR": _sb(128 * S),
    "HS": _sb(128 * S, "uint16"),
    "HR": _sb(128 * S, "uint16"),
    "OU": _sb(128 * (S + 1), "uint16"),
    "ZS": _sb(192 * (S + 1), "bfloat16"),
    "NS": _sb(128 * (S + 1)),
}
for _n in ("pUA", "pUB", "pUC", "pPA", "pPB", "pR", "pM", "pS"):
    SCRATCH[_n] = ("psum", [128, 512], "float32")
PIECE = {"%s%d" % (k, s): (k, SCRATCH[k][1][1] // n * s) for k, n in
         (("ZR", S), ("NR", S), ("HS", S), ("HR", S), ("OU", S + 1), ("ZS", S + 1), ("NS", S + 1)) for s in range(n)}
RECV = ("rO", "rZ", "rA", "rB", "rC", "rN")
DMAS = ["d_px", "d_ol", "d_z", "d_tl", "d_nl", "d_th", "d_x", "d_lo", "d_hi",
        "o_x", "o_lo", "o_hi", "o_pf", "o_p", "o_z", "o_n", "o_t"]
SEMAPHORES = ["v", "a", "t", "p", "loc"] + ["%s%d" % (k, s) for s in range(S) for k in RECV] + DMAS
HP = ((0, 64, "pUA", "rA"), (64, 96, "pUB", "rB"), (96, 128, "pUC", "rC"))
KB = ("pUA", "pUB")
PB = ("pPA", "pPB")
A0 = -8388608.0 - 1184.0


def rank_program(g, core, T, topo):
    rank = T.rank_of(core)
    if rank is None:
        return
    nxt = T.cores[(rank + 1) % len(T.cores)]
    prv = T.cores[(rank - 1) % len(T.cores)]
    queues = {"v": g.vector, "a": g.scalar, "t": g.tensor, "p": g, "s": g.sync}
    count = {"v": 0, "a": 0, "t": 0, "p": 0}
    seen = {q: {} for q in queues}
    acc = {}
    psum = set(n for n in SCRATCH if SCRATCH[n][0] == "psum")

    def need(q, regs, write, needs):
        for (n, lo, hi) in regs:
            for (qa, sem, val, alo, ahi, aw) in acc.get(n, ()):
                apart = ahi <= lo or alo >= hi
                if n in psum and qa != q:
                    apart = False
                elif apart or not (aw or write) or (qa == q and write and q == "t"):
                    continue
                needs[sem] = max(needs.get(sem, 0), val)

    def note(q, sem, val, regs, write):
        for (n, lo, hi) in regs:
            old = acc.get(n, [])
            if write:
                old = [a for a in old if not (lo <= a[3] and a[4] <= hi)]
            acc[n] = old + [(q, sem, val, lo, hi, write)]

    def waits(q, rd, wr):
        needs = {}
        need(q, rd, False, needs)
        need(q, wr, True, needs)
        for sem in sorted(needs):
            if seen[q].get(sem, 0) < needs[sem]:
                queues[q].wait_ge(T.sem[sem], needs[sem])
                seen[q][sem] = needs[sem]

    def regs(views):
        return [r for v in views for r in v[1]]

    def op(q, call, rd, wr):
        rd, wr = regs(rd), regs(wr)
        waits(q, rd, wr)
        count[q] += 1
        call().then_inc(T.sem[q], 1)
        note(q, q, count[q], rd, False)
        note(q, q, count[q], wr, True)

    def dma(q, sem, out, in_):
        waits(q, in_[1], out[1])
        queues[q].dma_start(out=out[0], in_=in_[0]).then_inc(T.sem[sem], 16)
        note("d" + sem, sem, 16, in_[1], False)
        note("d" + sem, sem, 16, out[1], True)

    sent = [0]

    def send(dst_name, src_name, lo, hi, sem):
        src, dst = V(src_name, lo, hi), V(dst_name, lo, hi)
        waits("p", src[1], [])
        rid, pid, _ = topo.addr(nxt)
        g.remote_dma(out_ap=dst[0], in_ap=src[0], remote_sem=T.sem[sem], local_sem=T.sem["loc"],
                     pid=pid, routing_id=rid, dma_engine_mask=topo.mask(core, nxt))
        sent[0] += len(topo.engines(core, nxt))
        note("r", sem, len(topo.engines(prv, core)), dst[1], True)

    def V(name, lo, hi, st=1):
        if name in PIECE:
            name, base = PIECE[name]
            lo, hi = lo + base, hi + base
        return (T[name][:, lo:hi] if st == 1 else T[name][:, lo:hi:st], [(name, lo, hi)])

    def ALL(name):
        return (T[name][:], [(name, 0, SCRATCH[name][1][1] if name in SCRATCH else 1)])

    def IND(win, off):
        return (win[0].indirect(off[0]), win[1] + off[1])

    def cols(*vs):
        return [v for v in vs if not isinstance(v, (int, float)) and v is not None]

    def raw(v):
        return v if isinstance(v, (int, float)) or v is None else v[0]

    def tt(o, a, b, f):
        op("v", lambda: g.vector.tensor_tensor(out=o[0], in0=a[0], in1=b[0], op=f), [a, b], [o])

    def ts(o, a, s1, f1, s2=None, f2=None):
        if f2 is None:
            op("v", lambda: g.vector.tensor_scalar(out=o[0], in0=a[0], scalar1=raw(s1), scalar2=None, op0=f1), [a] + cols(s1), [o])
        else:
            op("v", lambda: g.vector.tensor_scalar(out=o[0], in0=a[0], scalar1=raw(s1), scalar2=raw(s2), op0=f1, op1=f2),
               [a] + cols(s1, s2), [o])

    def cp(o, a):
        op("v", lambda: g.vector.tensor_copy(out=o[0], in_=a[0]), [a], [o])

    def scan(o, d0, d1, f0, f1):
        op("v", lambda: g.vector.tensor_tensor_scan(out=o[0], data0=d0[0], data1=d1[0], initial=0.0, op0=f0, op1=f1), [d0, d1], [o])

    def fill(o, c):
        op("v", lambda: g.vector.memset(o[0], c), [], [o])

    def act(o, a, f=ACT.Copy):
        op("a", lambda: g.scalar.activation(out=o[0], in_=a[0], func=f), [a], [o])

    def line(o, a, scale, bias):
        op("a", lambda: g.scalar.activation(out=o[0], in_=a[0], func=ACT.Identity, bias=raw(bias), scale=scale), [a] + cols(bias), [o])

    def mm(o, l, r, start=True, stop=True):
        op("t", lambda: g.tensor.matmul(out=o[0], lhsT=l[0], rhs=r[0], start=start, stop=stop), [l, r], [o])

    def iota(o, pattern, base, cm):
        op("p", lambda: g.iota(o[0], pattern, base, cm, allow_small_or_imprecise_dtypes=True), [], [o])

    def select(o, a, pattern, f, base, cm):
        op("p", lambda: g.affine_select(o[0], a[0], pattern, f, 0.0, base, cm), [a], [o])

    XR, PR = V("XW", 0, 4112), V("PW", 0, 4112)
    XA, PA = V("XW", 0, PADW), V("PW", 0, PADW)

    def tile(name, src, steps=(0, 16, 32, 64)):
        t = T[name]
        for w in steps:
            if w == 0:
                act((t[:, :, 0:16], [(name, 0, 16)]), V(src, 0, 64))
            else:
                act((t[:, :, w:2 * w], [(name, w, 2 * w)]), (t[:, :, 0:w], [(name, 0, w)]))

    def tile_end(name, copy):
        t = T[name]
        copy((t[:, :, 128:256], [(name, 128, 256)]), (t[:, :, 0:128], [(name, 0, 128)]))

    def pgather(a, b):
        return V("PG", 16 * a, 16 * b), IND(PR, V("OM", a, b))

    def reduce16(src, c0, c1, w, bank, first):
        out = V(bank, 0, c1 - c0)
        if first is not None:
            mm(out, first[0], first[1], True, False)
        for i in range(16):
            mm(out, V(w, 128 * i, 128 * i + 128), (T[src][:, 16 * c0 + i:16 * c1:16], [(src, 16 * c0, 16 * c1)]),
               first is None and i == 0, i == 15)

    def gather_abs(L, j, off, tname):
        lo = 512 * L + TW * j
        tt(V("DF", lo, lo + TW), IND(XR, V(off, lo // 16, (lo + TW) // 16)), (T[tname][:, L, 0:TW], [(tname, 0, TW)]), ALU.subtract)
        act(V("AB", lo, lo + TW), V("DF", lo, lo + TW), ACT.Abs)

    def h_of(piece, s, between=None):
        a, b, bank, sem = HP[piece]
        u = V(bank, 0, b - a)
        tt(V("hm", a, b), u, V("OQ%d" % (s % 2), a, b), ALU.mult)
        tt(V("pS", 256 + a, 256 + b), u, V("Q32", a, b), ALU.add)
        if between is not None:
            between()
        tt(V("hv", a, b), V("pS", 256 + a, 256 + b), V("hm", a, b), ALU.add)
        ts(V("hs", a, b), V("hv", a, b), 5, ALU.arith_shift_right, 4095, ALU.bitwise_and)
        ts(V("HS%d" % s, a, b), V("hs", a, b), 1.0, ALU.add)
        send("HR%d" % s, "HS%d" % s, a, b, "%s%d" % (sem, s))

    dma("s", "d_px", V("pxi", 0, 256), ALL("px"))
    dma("a", "d_ol", V("oli", 0, 128), ALL("ol"))
    dma("s", "d_z", V("ZS0", 0, 64), ALL("z"))
    dma("a", "d_tl", V("tli", 0, 128), ALL("tl"))
    fill(V("ones", 0, 128), 1.0)
    fill(V("XW", 0, 16), 0.0)
    fill(V("XW", 4096, PADW), 0.0)
    dma("s", "d_x", V("XW", 1, 4097), ALL("x"))
    dma("a", "d_nl", V("nli", 0, 128), ALL("nl"))
    dma("a", "d_th", ALL("thi"), ALL("th"))
    iota(V("pidx", 0, 1), [[0, 1]], 0, 1)
    select(V("G1", 0, 128), V("ones", 0, 128), [[-16, 8], [0, 16]], ALU.is_ge, 0, 1)
    select(V("GM", 0, 128), V("G1", 0, 128), [[16, 8], [0, 16]], ALU.is_ge, 15, -1)
    select(V("ID", 0, 128), V("ones", 0, 128), [[1, 128]], ALU.is_equal, 0, -1)
    iota(V("W", 0, 2048), [[0, 2048]], 0, 0)
    fill(V("PW", 0, PADW), 0.0)
    ts(V("LH", 256, 512), V("pxi", 0, 256), 1, ALU.add)
    waits("a", [("LH", 256, 512), ("PW", 0, PADW)], [])
    g.scalar.dma_start(out=T["PW"][1:128:16, 1:4097], in_=T["LH"][:, 256:512]).then_inc(T.sem["d_hi"], 16)
    ts(V("pxt", 0, 256), V("pxi", 0, 256), 1, ALU.add)
    ts(V("p16i", 0, 1), V("pidx", 0, 1), 15, ALU.bitwise_and)
    tt(V("LH", 0, 256), V("pxt", 0, 256), V("LH", 256, 512), ALU.subtract)
    dma("s", "d_lo", (T["PW"][0:128:16, 1:4097], [("PW", 1, 4097)]), V("LH", 0, 256))
    note("dd_hi", "d_hi", 16, [("LH", 256, 512)], False)
    acc["PW"] = acc["PW"] + [("dd_hi", "d_hi", 16, 1, 4097, True)]
    cp(V("p16", 0, 1), V("p16i", 0, 1))
    for L in range(4):
        cp(V("ZS0", 64 + 32 * L, 96 + 32 * L), V("tli", L, 128, 4))
    ts(V("q0", 0, 1), V("p16", 0, 1), 0.0, ALU.is_equal)
    ts(V("q1", 0, 1), V("p16", 0, 1), 1.0, ALU.is_equal)
    for L in range(4):
        ts(V("OW0", 32 * L, 32 * L + 32), V("oli", L, 128, 4), 1, ALU.add)
    ts(V("pS", 384, 512), V("ZS0", 64, 192), 0.0, ALU.is_gt)
    tt(V("wp", 0, 1), V("q1", 0, 1), V("q0", 0, 1), ALU.add)
    ts(V("GA", 0, 8), V("GM", 0, 128, 16), 32.0, ALU.mult)
    tt(V("om", 0, 128), V("pS", 384, 512), V("OW0", 0, 128), ALU.mult)
    ts(V("GP", 0, 8), V("GM", 0, 128, 16), V("wp", 0, 1), ALU.mult)
    fill(V("WP", 0, 2048), 0.0)
    cp(V("OM", 0, 128), V("om", 0, 128))
    ts(V("pS", 256, 384), V("ZS0", 64, 192), 0.0, ALU.is_le)
    for i in range(16):
        cp(V("WP", 128 * i + i, 128 * i + 128, 16), V("GP", 0, 8))
    for L in range(4):
        ts(V("NS0", 32 * L, 32 * L + 32), V("nli", L, 128, 4), 1, ALU.add)
    cp(V("OU0", 0, 128), V("OW0", 0, 128))
    tt(V("NM", 0, 128), V("pS", 256, 384), V("NS0", 0, 128), ALU.mult)
    tile("ztb", "ZS0")
    tile_end("ztb", act)
    act(*pgather(0, 64))
    cp(*pgather(64, 128))
    for i in range(16):
        act(V("W", 128 * i + i, 128 * i + 128, 16), V("GA", 0, 8))
    select(V("LT", 0, 128), V("GM", 0, 128), [[1, 128]], ALU.is_gt, 0, -1)
    iota(V("mod16", 0, 128), [[0, 8], [1, 16]], 0, 0)
    iota(V("colc", 0, 128), [[1, 128]], 0, 0)
    iota(V("dump0", 0, 8), [[0, 2], [16, 4]], DUMP0, 0)
    iota(V("dumpw", 0, 128), [[16, 4], [0, 32]], DUMP0, 0)
    select(V("SEG16", 0, 128), V("ones", 0, 128), [[0, 8], [1, 16]], ALU.is_gt, 0, 0)
    select(V("SEG32", 0, 128), V("ones", 0, 128), [[0, 4], [1, 32]], ALU.is_gt, 0, 0)
    select(ALL("GE1"), (T["ones"][0:8, 0:128], [("ones", 0, 128)]), [[1, 128]], ALU.is_ge, 0, -16)
    select(ALL("GE"), ALL("GE1"), [[-1, 128]], ALU.is_ge, 15, 16)

    def late_constants():
        cp(ALL("thf"), ALL("thi"))
        fill(ALL("oneb"), 1.0)
        mm(V("pM", 128, 133), ALL("GE"), ALL("thf"))
        line(ALL("CQ"), (T["colc"][0:1, 0:128], [("colc", 0, 128)]), -0.25, 31.75)
        line(V("C2", 0, 128), V("colc", 0, 128), -0.5, 130560.0 + 63.5)
        ts(V("DM", 0, 128), V("mod16", 0, 128), V("p16", 0, 1), ALU.is_equal)
        ts(V("ND", 0, 128), V("mod16", 0, 128), V("p16", 0, 1), ALU.not_equal)
        fill(V("ND", 128, 144), 1.0)
        ts(V("dump", 0, 8), V("dump0", 0, 8), V("p16", 0, 1), ALU.add)
        ts(V("OW1", 128, 256), V("dumpw", 0, 128), V("p16", 0, 1), ALU.add)
        ts(V("OW0", 128, 256), V("dumpw", 0, 128), V("p16", 0, 1), ALU.add)
        fill(V("GD", 192, 208), 0.0)
        ts(V("LM", 0, 5), V("pM", 128, 133), 32.0, ALU.mult, 31.75, ALU.add)

    for s in range(S):
        par, nxp = s % 2, (s + 1) % 2
        last = s == S - 1
        zr, nr, hr, zs1 = "ZR%d" % s, "NR%d" % s, "HR%d" % s, "ZS%d" % (s + 1)
        send("OU%d" % (s + 1), "OU%d" % s, 0, 128, "rO%d" % s)
        send(zr, "ZS%d" % s, 0, 192, "rZ%d" % s)
        for half in (0, 1):
            a, b = 64 * half, 64 * half + 64
            reduce16("PG", a, b, "WP", PB[half], (V("ID", 0, 128), V("NM", a, b)))
            if half == 0 and s > 0:
                mm(V("pM", 136, 137), V("GM", 0, 128), V("rs", 0, 1))
        cp(V("RU", 0, 64), V(PB[0], 0, 64))
        for L in (0, 1):
            for j in (0, 1):
                gather_abs(L, j, "RU", "ztb")
        reduce16("AB", 0, 64, "W", "pUA", None)
        if s > 0:
            line(V("A32", 0, 1), V("pM", 136, 137), 32.0, A0)
            line(V("Q32", 0, 128), V("OW%d" % par, 0, 128), 1184.0, V("A32", 0, 1))
            tt(V("pS", 128, 256), V("pS", 0, 128), V("hN", 0, 128), ALU.mult)
            cp(V("RU", 64, 128), V(PB[1], 0, 64))
            tt(V("NS%d" % s, 0, 128), V("pS", 128, 256), V("NR%d" % (s - 1), 0, 128), ALU.add)
        else:
            line(V("OQ0", 0, 128), V("OW0", 0, 128), 1.0 / 32, -1.0 / 32)
            line(V("Q32", 0, 128), V("OW0", 0, 128), 1184.0, A0)
            cp(V("RU", 64, 128), V(PB[1], 0, 64))
        for j in (0, 1):
            gather_abs(2, j, "RU", "ztb")
            if s > 0:
                tile("ztc", zr, ((0,), (16,))[j])
        reduce16("AB", 64, 96, "W", "pUB", None)
        gather_abs(3, 0, "RU", "ztb")
        if s > 0:
            tile("ztc", zr, (32,))
        h_of(0, s, lambda: gather_abs(3, 1, "RU", "ztb"))
        reduce16("AB", 96, 128, "W", "pUC", None)
        tile("ztc", zr, (64,) if s > 0 else (0, 16, 32, 64))
        tile_end("ztc", act)
        h_of(1, s)
        date = V(zr, 64, 192)
        if s == 0:
            late_constants()

        def known():
            cp(V("OW%d" % nxp, 0, 128), V("OU%d" % (s + 1), 0, 128))
            ts(V("e1", 0, 128), date, float(s), ALU.is_gt, -BIG, ALU.mult)
            ts(V("e2", 0, 128), date, 99.0, ALU.is_lt)

        if s > 0:
            known()
        h_of(2, s)
        send(nr, "NS%d" % s, 0, 128, "rN%d" % s)
        if s == 0:
            known()
        if last:
            dma("s", "o_lo", V("LO", 0, 256), (T["PW"][0:128:16, 1:4097], [("PW", 1, 4097)]))
            dma("s", "o_hi", V("LO", 256, 512), (T["PW"][1:128:16, 1:4097], [("PW", 1, 4097)]))
        line(V("OQ%d" % nxp, 0, 128), V("OW%d" % nxp, 0, 128), 1.0 / 32, -1.0 / 32)
        line(V("ST", 0, 128), date, -1.0, float(s + 2))
        for half in (0, 1):
            a, b = 64 * half, 64 * half + 64
            for L in (2 * half, 2 * half + 1):
                for j in (0, 1):
                    gather_abs(L, j, hr, "ztc")
            if last and half == 0:
                line(V("pR", 256, 512), V("LO", 256, 512), 1.0, -1.0)
            reduce16("AB", a, b, "W", KB[half], (ALL("oneb"), (T["CQ"][:, a:b], [("CQ", a, b)])))
        cp(V("HW", 0, 128), V(hr, 0, 128))

        def keys(half, between=None):
            a, b = 64 * half, 64 * half + 64
            kd = V(KB[half], 0, 64)
            tt(V("K2", a, b), V("C2", a, b), kd, ALU.subtract)
            scan(V("SM", a, b), V("SEG32", a, b), kd, ALU.mult, ALU.max)
            if between is not None:
                between()
            scan(V("SM", 128 + a, 128 + b), V("SEG32", a, b), V("K2", a, b), ALU.mult, ALU.max)

        def redeem(half, n):
            a, b = 64 * half, 64 * half + 64
            if n == 0:
                tt(V("pS", a, b), V(KB[half], 0, 64), V("RT", a, b), ALU.is_le)
            elif n == 1:
                tt(V("pS", 128 + a, 128 + b), V("pS", a, b), V("ST", a, b), ALU.mult)
            else:
                tt(V("pS", 256 + a, 256 + b), V("pS", 128 + a, 128 + b), V(zr, 64 + a, 64 + b), ALU.add)

        def refuse(L):
            ts(V("RF", 32 * L, 32 * L + 32), V(KB[L // 2], 32 * (L % 2), 32 * (L % 2) + 32), V("gk", L, L + 1),
               ALU.is_equal, 99.0, ALU.mult)

        def newdate(half):
            a, b = 64 * half, 64 * half + 64
            tt(V(zs1, 64 + a, 64 + b), V("pS", 256 + a, 256 + b), V("RF", a, b), ALU.max)

        def onward(n):
            if last:
                return
            if n == 0:
                ts(V("pS", 384, 512), V(zs1, 64, 192), float(s + 1), ALU.is_gt)
            elif n == 1:
                ts(V("pS", 256, 384), V(zs1, 64, 192), float(s + 1), ALU.is_le)
            elif n == 2:
                tt(V("om", 0, 128), V("pS", 384, 512), V("OW%d" % nxp, 0, 128), ALU.mult)
            elif n == 3:
                cp(V("OM", 0, 128), V("om", 0, 128))
            else:
                tt(V("NM", 0, 128), V("pS", 256, 384), V(nr, 0, 128), ALU.mult)

        def write(L, win, fu, data):
            cp(IND(win, V("fu", fu + 2 * L, fu + 2 * L + 1)), V(data, 16 * L, 16 * L + 16))

        if last:
            tt(V("YPg", 0, 256), V("pR", 256, 512), V("LO", 0, 256), ALU.add)
            dma("s", "o_pf", (T["PF"][0:128:16, 1:4097], [("PF", 1, 4097)]), V("YPg", 0, 256))
        tt(V("RT0", 0, 128), V("e1", 0, 128), V("e2", 0, 128), ALU.mult)
        keys(0)
        ts(V("RT", 0, 128), V("RT0", 0, 128), V("LM", s, s + 1), ALU.add)
        tt(V("hN", 0, 128), V("HW", 0, 128), V(nr, 0, 128), ALU.subtract)
        for n in (0, 1, 2):
            redeem(0, n)
        keys(1, lambda: redeem(1, 0))
        lastk = V("SM", 31, 128, 32)
        ts(V("nogo", 0, 4), lastk, V("LM", s, s + 1), ALU.is_le, 128.0, ALU.mult)
        redeem(1, 1)
        ts(V("KI", 0, 8), V("SM", 31, 256, 32), 4.0, ALU.mult)
        ts(V("CI", 0, 8), V("KI", 0, 8), 127, ALU.bitwise_and)
        tt(V("gk", 0, 4), lastk, V("nogo", 0, 4), ALU.subtract)
        ts(V("OFF", 0, 8), V("CI", 0, 8), -1.0, ALU.mult, 127.0, ALU.add)
        tt(V("CI", 8, 12), V("CI", 0, 4), V("nogo", 0, 4), ALU.subtract)
        redeem(1, 2)
        tt(V("GD", 0, 128), IND(V("HW", 0, 128), V("OFF", 0, 8)), V("DM", 0, 128), ALU.mult)
        ts(V("OFF", 8, 12), V("CI", 8, 12), -1.0, ALU.mult, 127.0, ALU.add)
        refuse(0)
        tt(V("GD", 128, 192), IND(V("OW%d" % nxp, 0, 256), V("OFF", 8, 12)), V("DM", 0, 64), ALU.mult)
        mm(V("pM", 0, 128), V("LT", 0, 128), V("GD", 64, 192))
        mm(V("pR", 64, 128), V("GM", 0, 128), V("GD", 0, 64))
        scan(V("OWN", 0, 144), V("ND", 0, 144), V("GD", 64, 208), ALU.mult, ALU.add)
        refuse(1)
        cp(V("HB", 0, 4), V("OWN", 15, 64, 16))
        refuse(2)
        refuse(3)
        tt(V("gz", 0, 64), IND(XR, V("HB", 0, 4)), V(zr, 0, 64), ALU.add)
        tt(V("E", 0, 128), V("OWN", 16, 144), V("pM", 0, 128), ALU.is_equal)
        ts(V("zi", 0, 64), V("gz", 0, 64), 0.5, ALU.mult, -0.25, ALU.add)
        if not last:
            ts(V("hx", 0, 64), V("pR", 64, 128), V("q1", 0, 1), ALU.mult)
        scan(V("F", 0, 128), V("SEG16", 0, 128), V("E", 0, 128), ALU.mult, ALU.max)
        cp(V(zs1, 0, 64), V("zi", 0, 64))
        if not last:
            tile("ztb", zs1)
            tt(V("PD", 0, 64), V("pR", 64, 128), V("hx", 0, 64), ALU.subtract)
        else:
            dma("a", "o_z", ALL("yz"), V(zs1, 0, 64))
            ts(V("ht", 0, 64), V("pR", 64, 128), -1.0, ALU.add)
        tt(V("f1", 0, 8), V("F", 15, 128, 16), V("dump", 0, 8), ALU.mult)
        newdate(0)
        newdate(1)
        tt(V("f2", 0, 8), V("f1", 0, 8), V("OWN", 15, 128, 16), ALU.max)
        onward(0)
        cp(V("fu", 0, 16, 2), V("f2", 0, 8))
        onward(1)
        if not last:
            for L in (3, 2, 1, 0):
                write(L, PA, 8, "PD")
                if L:
                    onward(5 - L)
            act(*pgather(0, 32))
            cp(*pgather(32, 64))
            act(*pgather(64, 112))
            write(3, XA, 0, "zi")
            tile_end("ztb", cp)
            write(2, XA, 0, "zi")
            op("v", lambda: g.vector.tensor_reduce(out=T["rs"][:, 0:1], in_=T["pS"][:, 0:128], axis=AxisListType.X, op=ALU.add),
               [V("pS", 0, 128)], [V("rs", 0, 1)])
            write(1, XA, 0, "zi")
            cp(*pgather(112, 128))
            write(0, XA, 0, "zi")
        else:
            tt(V("pS", 128, 256), V("pS", 0, 128), V("hN", 0, 128), ALU.mult)
            for L in (3, 2, 1, 0):
                write(L, XA, 0, "zi")
                cp(V("YT", L, 128, 4), V(zs1, 64 + 32 * L, 96 + 32 * L))
            dma("s", "o_x", ALL("yx"), V("XW", 1, 4097))
            dma("a", "o_t", ALL("yt"), V("YT", 0, 128))
            tt(V("NS%d" % (s + 1), 0, 128), V("pS", 128, 256), V(nr, 0, 128), ALU.add)
            for L in (3, 2, 1, 0):
                write(L, V("PF", 0, PADW), 8, "ht")
                ts(V("YN", L, 128, 4), V("NS%d" % (s + 1), 32 * L, 32 * L + 32), -1.0, ALU.add)
            dma("a", "o_p", ALL("yp"), (T["PF"][0:128:16, 1:4097], [("PF", 1, 4097)]))
            dma("s", "o_n", ALL("yn"), V("YN", 0, 128))
    for q in ("v", "a", "t", "p"):
        g.wait_ge(T.sem[q], count[q])
    g.wait_ge(T.sem["loc"], sent[0])
    for n in DMAS:
        g.wait_ge(T.sem[n], 16)
    for s in range(S):
        for k in RECV:
            g.wait_ge(T.sem["%s%d" % (k, s)], len(topo.engines(prv, core)))
